import numpy as np, ml_dtypes
CORES = [16,32,48,64,80]
N = 5
import mx_ref
BF = ml_dtypes.bfloat16
def entries(a):
    return np.ascontiguousarray(a.T).reshape(-1)
def table(e):
    return np.ascontiguousarray(np.reshape(e, (-1, 16)).T).astype(np.int32)
def cols(t, e):
    v = np.concatenate([t.reshape(128, -1, 4), np.zeros((128, 1, 4), BF)], axis=1)
    return np.ascontiguousarray(v[:, e]).reshape(128, -1)
def cut(t, i, w=512):
    return t[:, w * i:w * i + w]
def f(rng, *shape):
    return mx_ref.flush((rng.standard_normal(shape, dtype=np.float32) * np.exp2(rng.integers(-2, 3, shape[:-1] + (1,)))).astype(BF))
def wide(rng, *shape, cols=0):
    v = rng.standard_normal(shape, dtype=np.float32) * np.exp2(rng.integers(-12, 13, shape)).astype(np.float32)
    if cols: v *= np.repeat(np.exp2(rng.integers(-cols, cols + 1, shape[:-2] + (1, shape[-1] // 4))) * (rng.random(shape[:-2] + (1, shape[-1] // 4)) > 0.0625), 4, axis=-1).astype(np.float32)
    return mx_ref.flush(v.astype(BF))
T, O = 384, 2
def places(rng, dest):
    e = np.zeros((N, T), int)
    for d in range(N): e[dest == d] = d * T + rng.permutation(T)
    return np.stack([table(e[r]) for r in range(N)])
def relabel(rng):
    p = rng.permutation(N)
    if np.all((p - np.arange(N)) % N == p[0]): p[[0, 1]] = p[[1, 0]]
    return p
def setup_inputs(rng):
    e = rng.permutation(N * T).reshape(N, T)
    return {"x": f(rng, N, 128, 4 * T), "to": np.stack([table(e[r]) for r in range(N)]), "w": f(rng, N, 128, 512 * O)}
def setup_inputs_swap(rng):
    d = setup_inputs(rng); p = rng.permutation(N); dest = np.zeros((N, T), int)
    for k in range(N): dest[p[k]] = p[(k + 1) % N]
    d["to"] = places(rng, dest); return d
def setup_inputs_ones(rng):
    d = setup_inputs(rng); i = np.arange(N); n = np.ones((N, N), int); n[i, rng.permutation(N)] += T % N
    for t in range(T // N - 1): n[i, rng.permutation(N)] += N
    d["to"] = places(rng, np.stack([rng.permutation(np.repeat(i, n[r])) for r in range(N)])); return d
def setup_inputs_runs(rng):
    d = setup_inputs(rng); p = relabel(rng); s, u = rng.integers(1, N), rng.integers(0, N); g, h = rng.permutation(N), rng.permutation(N)
    n = T // N + ((g[:, None] + h) % N < T % N)
    j = (np.arange(N) + s * np.arange(N)[:, None] + u) % N
    d["to"] = places(rng, np.stack([np.repeat(p[j[r]], n[r, j[r]]) for r in range(N)])); return d
def setup_inputs_comb(rng):
    d = setup_inputs(rng); p = relabel(rng); s, u = rng.integers(1, N), rng.integers(0, N); k = rng.permutation(N); c = np.arange(T)
    d["to"] = places(rng, np.stack([p[(c + np.where(c < T - T % N, s * r + u, k[r])) % N] for r in range(N)])); return d
def setup_inputs_spread(rng):
    d = setup_inputs(rng); d["x"] = wide(rng, N, 128, 4 * T, cols=8); return d
def check_inputs(d):
    e = np.concatenate([entries(d["to"][r]) for r in range(N)])
    return [] if np.array_equal(np.sort(e), np.arange(N * T)) else ["to"]
def reference(x, to, w):
    z = np.concatenate([x[r] for r in range(N)], axis=1)
    e = np.concatenate([entries(to[r]) for r in range(N)])
    home = np.zeros(N * T, int); home[e] = np.arange(N * T)
    y = np.zeros((N, 128, O * T), np.float32)
    for d in range(N):
        v = mx_ref.quantize(cols(z, home[d * T:d * T + T]))
        for o in range(O): y[d][:, T * o:T * o + T] = mx_ref.matmul(mx_ref.quantize(np.ascontiguousarray(cut(w[d], o))), v)
    return {"y": y}

@@ -1,0 +1,346 @@
+from concourse.bass import DstId, RemoteDMATransfer
+from concourse.mybir import dt, AluOpType, AxisListType, ActivationFunctionType
+
+N, COLS = 5, 384
+SLOT = 80
+SENT1 = 77
+H = 6
+W = COLS // H
+WHOLE = 3 << 22
+
+F32, BF, I32, U16 = "float32", "bfloat16", "int32", "uint16"
+X4, U8 = "float8_e4m3fn_x4", "uint8"
+SMALL = {
+    X4: "q:128,384 wq:128,256 q2:128,400 ql:128,400 q3:128,400 qm:128,400 q4:128,384",
+    U8: "p:128,384 wp:128,256 p2:128,400 pl:128,400 p3:128,400 pm:128,400 p4:128,384",
+    BF: "xt:128,1536 wt:128,1024 val1:128,192 win1:128,400 dup1:128,25,32 tr1:128,800 dup2:32,5,32 tr2:32,160 v3:32,64 "
+        "val3:128,384 win3:128,1920 dup3:128,24,32 tr3:128,768",
+    I32: "qf:128,192 e1:32,64 pp1:32,12 e2:32,384 ci2:32,30 e3:32,64 pp3:32,64 t3:128,32",
+    U16: "of1:128,12 l1:128,26 l2:128,26 of3:128,24 l3:128,24",
+    F32: "ys:128,768 cst:128,160 ct:128,160 fr:128,192 lm:32,32 tf:128,192 uf:128,192 ones:32,64 rst:32,25 ms2:32,50 tcon:32,80 "
+         "sam:32,30 lsa:32,30 ms3:32,25 kk8:32,25 a1:32,64 b1:32,64 i1:32,64 c1:32,64 g1:32,64 z1:32,64 zt1:32,64 ln1:32,32 "
+         "lt1:32,32 bs1:32,1 s1a:32,52 s1b:32,38 s1:32,12 y1:32,12 sm1:128,25 cm2:32,384 sg2:32,1 bm2:32,32 row2:32,32 "
+         "cn2:32,25 m2:32,50 sh2:32,25 mm2:32,50 ta2:32,40 tb2:32,35 tc2:32,30 seg:32,400 sa2:32,160 sb2:32,80 pk2:32,25 a3:32,64 "
+         "b3:32,64 c3:32,64 na3:32,1 nb3:32,64 la3:32,30 lb3:32,30 lc3:32,32 lt3:32,32 bs3:32,1 g3:32,64 k3:32,64 cx3:32,5,10 "
+         "cr3:32,5,10 cn3:32,25 in3:32,25 x3:32,25 xt3:32,5 xs3:32,10 sg3:32,320 sa3:32,128 sb3:32,64 tq3:128,64 sm3:128,24 "
+         "su3:32,72",
+}
+SCRATCH = {"ps": ("psum", [128, 2048], F32), "lists": ("dram", [N, 128, 3], I32)}
+for _t in SMALL:
+    for _b in SMALL[_t].split():
+        SCRATCH[_b.split(":")[0]] = ("sbuf", [int(_n) for _n in _b.split(":")[1].split(",")], _t)
+SEMAPHORES = ["v", "gs", "d_e1", "d_x", "d_w", "d_l", "d_e2", "d_e3", "d_t3", "d_o1", "d_v3", "d_o2",
+              "sl", "s1c", "s1p", "s2c", "s2p", "loc", "ap", "m0", "m1", "m2", "m3", "ac", "st", "st2"]
+
+
+def rank_program(g, core, T, topo):
+    me = T.rank_of(core)
+    if me is None:
+        return
+    S, V, A = T.sem, g.vector, g.scalar
+    op = AluOpType
+    X, COPY, LINE = AxisListType.X, ActivationFunctionType.Copy, ActivationFunctionType.Identity
+    others = [r for r in range(N) if r != me]
+    cnt = {"v": 0, "gs": 0, "ac": 0}
+
+    def v(name, *args):
+        if cnt["v"]:
+            V.wait_ge(S.v, cnt["v"])
+        calls = {"ts": V.tensor_scalar, "tt": V.tensor_tensor, "cp": V.tensor_copy, "ms": V.memset, "red": V.tensor_reduce,
+                 "scan": V.tensor_tensor_scan, "tr": V.transpose, "qz": V.quantize_mx}
+        calls[name](*args).then_inc(S.v, 1)
+        cnt["v"] += 1
+        return cnt["v"]
+
+    def ts(out, a, s1, o1, s2=None, o2=None):
+        return v("ts", out, a, s1, s2, o1) if o2 is None else v("ts", out, a, s1, s2, o1, o2)
+
+    def tt(out, a, b, o):
+        return v("tt", out, a, b, o)
+
+    def act(out, in_, func, **k):
+        if cnt["ac"]:
+            A.wait_ge(S.ac, cnt["ac"])
+        A.activation(out, in_, func, **k).then_inc(S.ac, 1)
+        cnt["ac"] += 1
+        return cnt["ac"]
+
+    def gc(call, *args, **k):
+        if cnt["gs"]:
+            g.wait_ge(S.gs, cnt["gs"])
+        call(*args, **k).then_inc(S.gs, 1)
+        cnt["gs"] += 1
+        return cnt["gs"]
+
+    def iota(out, pattern, base=0, cm=0):
+        return gc(g.iota, out, pattern, base, cm, allow_small_or_imprecise_dtypes=True)
+
+    def sel(out, in_, pattern, how, base, cm):
+        return gc(g.affine_select, out, in_, pattern, how, 0.0, base, cm)
+
+    for d in range(N):
+        (g.sync if d % 2 else A).dma_start(T.e1[H * d:H * d + H, :], T.to[:]).then_inc(S.d_e1, 16)
+    g.sync.dma_start(T.lists[me], T.to[:]).then_inc(S.d_l, 16)
+    g.sync.dma_start(T.xt[:, 0:768], T.x[:, 0:768]).then_inc(S.d_x, 16)
+    A.dma_start(T.xt[:, 768:1536], T.x[:, 768:1536]).then_inc(S.d_x, 16)
+    g.sync.dma_start(T.wt[:], T.w[:]).then_inc(S.d_w, 16)
+
+    v("ms", T.cst[:], 0.0)
+    v("ms", T.z1[:], 0.0)
+    v("ms", T.ln1[:], 0.0)
+    v("ms", T.win1[:], 0.0)
+    g.wait_ge(S.v, 1)
+    iota(T.cst[0:32, 32:62], [[COLS, N], [0, H]])
+    iota(T.cst[0:32, 64:94], [[COLS, N], [0, H]], COLS)
+    iota(T.cst[0:32, 96:126], [[COLS, N + 1], [0, N]])
+    iota(T.cst[0:32, 128:158], [[0, N + 1], [5 * SLOT, N]])
+    rows = iota(T.cst[:, 0:32], [[32, 2], [0, 16]])
+    order = iota(T.fr[:], [[64, 2], [2 * W, H], [2, 16]], -23)
+    iota(T.ones[:], [[0, 64]], 1)
+    tri = sel(T.lm[:], T.ones[:, 0:32], [[1, 32]], op.is_gt, 0, -1)
+    V.wait_ge(S.gs, rows)
+    v("tr", T.ct[:], T.cst[:])
+    V.wait_ge(S.gs, order)
+    ts(T.qf[:], T.fr[:], T.ct[:, 0:1], op.add, 1.0 / 48, op.mult)
+    ts(T.tf[:], T.fr[:], T.ct[:, 0:1], op.add, 8.0, op.mult)
+    ts(T.uf[:], T.qf[:], -383.0, op.mult, -8.0, op.add)
+    tt(T.val1[:], T.tf[:], T.uf[:], op.add)
+
+    per = len(topo.engines(core, T.cores[others[0]])) // len(others)
+    landed = per * len(others)
+
+    def spread(src, dst, sem):
+        moves = []
+        for i, r in enumerate(others):
+            rid, pid, _ = topo.addr(T.cores[r])
+            e = topo.engines(core, T.cores[r])[per * i:per * i + per]
+            moves.append(RemoteDMATransfer(dst_ids=[DstId(rid=rid, pnc=pid)], dma_engine_mask=sum(1 << b for b in e),
+                                           remote_sem=sem, srcs=[src(r)], dsts=[dst]))
+        g.remote_dma_fused(moves, local_sem=S.loc)
+    g.wait_ge(S.d_l, 16)
+    spread(lambda r: T.lists[me], T.lists[me], S.sl)
+
+    t0 = iota(T.t3[:], [[0, 32]])
+    iota(T.bm2[:], [[0, 32]])
+    sel(T.rst[:], T.ones[:, 0:25], [[0, 5], [1, 5]], op.is_gt, 0, 0)
+    sel(T.ms2[:], T.ones[:, 0:50], [[0, 2], [1, 5], [0, 5]], op.is_equal, 0, -1)
+    tables = iota(T.tcon[:], [[1, SLOT]])
+    iota(T.lc3[:], [[0, 32]])
+    sel(T.lb3[:], T.ones[:, 0:30], [[-H, 5], [0, H]], op.is_ge, 0, 1)
+    sel(T.sam[:], T.lb3[:], [[H, 5], [0, H]], op.is_ge, H - 1, -1)
+    sel(T.lsa[:], T.sam[:], [[1, 30]], op.is_gt, 0, -1)
+    sel(T.cn3[:], T.ones[:, 0:25], [[0, 5], [-H, 5]], op.is_ge, 0, 1)
+    sel(T.ms3[:], T.cn3[:], [[0, 5], [H, 5]], op.is_ge, H - 1, -1)
+    iota(T.kk8[:], [[SLOT, 5], [SLOT, 5]], WHOLE - 200)
+    iota(T.val3[:], [[0, COLS]])
+    more = iota(T.win3[:, COLS * me:COLS * me + COLS], [[0, COLS]])
+
+    R = slice(0, 30)
+    V.wait_ge(S.d_e1, 80)
+    ts(T.a1[R, :], T.e1[R, :], T.ct[R, 32:33], op.is_ge)
+    ts(T.b1[R, :], T.e1[R, :], T.ct[R, 64:65], op.is_ge)
+    v("scan", T.c1[R, :], T.a1[R, :], T.b1[R, :], 0.0, op.add, op.subtract)
+    V.wait_ge(S.gs, tri)
+    ts(T.ln1[R, :], T.lm[R, :], T.c1[R, W - 1:W], op.mult)
+    v("tr", T.lt1[:], T.ln1[:])
+    v("red", T.bs1[:], T.lt1[:], X, op.add)
+    tt(T.i1[R, :], T.a1[R, :], T.b1[R, :], op.subtract)
+    ts(T.g1[R, :], T.c1[R, :], T.bs1[R, 0:1], op.add, float(SLOT), op.mult)
+    tt(T.z1[R, :], T.g1[R, :], T.i1[R, :], op.mult)
+    v("tr", T.zt1[:], T.z1[:])
+    tt(T.s1a[:], T.zt1[:, 0:52], T.zt1[:, 12:64], op.add)
+    tt(T.s1b[:], T.s1a[:, 0:38], T.s1a[:, 6:44], op.add)
+    tt(T.s1[:, 0:6], T.s1b[:, 0:6], T.zt1[:, 24:30], op.add)
+    tt(T.s1[:, 6:12], T.s1b[:, 32:38], T.zt1[:, 56:62], op.add)
+    ts(T.pp1[:], T.s1[:], 0.2 / SLOT, op.mult, -0.6, op.add)
+    ts(T.y1[:], T.pp1[:], float(1 - 5 * SLOT), op.mult, -float(SLOT), op.add)
+    tt(T.s1[:], T.s1[:], T.y1[:], op.add)
+    for a in range(4):
+        v("cp", T.of1[32 * a:32 * a + 32, :], T.s1[:])
+    v("cp", T.win1[:, 0:400].indirect(T.of1[:, 0:12]), T.val1[:])
+    v("cp", T.dup1[:, :, 0:16], T.win1[:])
+    v("cp", T.dup1[:, :, 16:32], T.win1[:])
+    v("tr", T.tr1[:], T.dup1[:])
+    tt(T.sm1[:], T.tr1[:, 0:800:32], T.tr1[:, 16:800:32], op.add)
+    ts(T.l1[:, 0:25], T.sm1[:], 192.0, op.add)
+    V.wait_ge(S.d_x, 32)
+    n1 = v("qz", T.q[:], T.p[:], T.xt[:])
+    k1 = v("cp", T.q2[:].bitcast(dt.uint32), T.q[:].bitcast(dt.uint32).indirect(T.l1[:, 0:25]))
+    A.wait_ge(S.v, n1)
+    A.activation(T.p2[:], T.p[:].indirect(T.l1[:, 0:25]), COPY).then_inc(S.ap, 1)
+
+    cut = lambda r, n: slice(SLOT * r, SLOT * r + n)
+    g.wait_ge(S.v, k1)
+    spread(lambda r: T.q2[:, cut(r, SENT1)].bitcast(dt.uint8), T.ql[:, cut(me, SENT1)].bitcast(dt.uint8), S.s1c)
+    g.wait_ge(S.ap, 1)
+    spread(lambda r: T.p2[:, cut(r, SENT1)], T.pl[:, cut(me, SENT1)], S.s1p)
+
+    g.sync.wait_ge(S.sl, landed)
+    g.sync.wait_ge(S.d_l, 16)
+    for d in range(N + 1):
+        g.sync.dma_start(T.e2[N * d:N * d + N, :], T.lists[:]).then_inc(S.d_e2, 16)
+    g.sync.dma_start(T.e3[R, :], T.lists[:]).then_inc(S.d_e3, 16)
+    g.sync.wait_ge(S.gs, t0)
+    for b in range(8):
+        g.sync.dma_start(T.t3[32 * (b // 2):32 * (b // 2) + 24, 16 * (b % 2):16 * (b % 2) + 16], T.lists[b % N]).then_inc(S.d_t3, 16)
+    g.sync.wait_ge(S.v, k1)
+    g.sync.dma_start(T.ql[:, cut(me, SLOT)].bitcast(dt.uint8), T.q2[:, cut(me, SLOT)].bitcast(dt.uint8)).then_inc(S.d_o1, 16)
+    g.sync.wait_ge(S.ap, 1)
+    g.sync.dma_start(T.pl[:, cut(me, SLOT)], T.p2[:, cut(me, SLOT)]).then_inc(S.d_o1, 16)
+
+    V.wait_ge(S.d_e2, 96)
+    V.wait_ge(S.gs, tables)
+    ts(T.cm2[R, :], T.e2[R, :], T.ct[R, 96:97], op.is_ge)
+    v("red", T.sg2[R, :], T.cm2[R, :], X, op.add)
+    ts(T.bm2[R, :], T.ones[R, 0:32], T.sg2[R, 0:1], op.mult, T.ct[R, 128:129], op.subtract)
+    nrow = v("tr", T.row2[:], T.bm2[:])
+    ts(T.ci2[:], T.row2[:, 0:30], -0.2, op.mult, (386 - me) * 0.2, op.add)
+    tt(T.cn2[:], T.ci2[:, 5:30], T.ci2[:, 0:25], op.subtract)
+    v("scan", T.m2[:, 0:25], T.rst[:], T.cn2[:], 0.0, op.mult, op.add)
+    tt(T.sh2[:], T.ci2[:, 4:29], T.rst[:], op.mult)
+    tt(T.m2[:, 25:50], T.ci2[:, 0:25], T.sh2[:], op.subtract)
+    tt(T.mm2[:], T.m2[:], T.ms2[:], op.mult)
+    tt(T.ta2[:], T.mm2[:, 0:40], T.mm2[:, 10:50], op.add)
+    tt(T.tb2[:], T.ta2[:, 0:35], T.ta2[:, 5:40], op.add)
+    tt(T.tc2[:], T.tb2[:, 0:30], T.mm2[:, 20:50], op.add)
+    ts(T.seg[:, 0:SLOT], T.tcon[:], T.tc2[:, 25:26], op.add)
+    for r in range(1, N):
+        ts(T.seg[:, SLOT * r:SLOT * r + SLOT], T.tcon[:], T.tc2[:, r - 1:r], op.is_ge, T.tc2[:, 25 + r:26 + r], op.mult)
+    tt(T.sa2[:], T.seg[:, 0:160], T.seg[:, 160:320], op.add)
+    tt(T.sb2[:], T.sa2[:, 0:80], T.sa2[:, 80:160], op.add)
+    tt(T.sb2[:], T.sb2[:], T.seg[:, 320:400], op.add)
+    last = float(SLOT * (N - 1) + SENT1 - 1)
+    ts(T.dup2[:, :, 0:16], T.sb2[:], last, op.min, -200.0, op.add)
+    ts(T.dup2[:, :, 16:32], T.sb2[:], last, op.min, -200.0, op.add)
+    nt2 = v("tr", T.tr2[:], T.dup2[:])
+
+    A.wait_ge(S.v, nrow)
+    for k in range(N):
+        act(T.cx3[:, k, :], T.row2[:, 5 * me:5 * me + 10], LINE, scale=-0.2, bias=(386 - k) * 0.2)
+    nc3 = act(T.cr3[:], T.cx3[:], LINE, bias=float(WHOLE))
+    A.wait_ge(S.v, nt2)
+    for d in (3, 4):
+        npk = act(T.pk2[:, 5 * d:5 * d + 5], T.tr2[:, d:160:32], COPY)
+    for d in range(3):
+        v("cp", T.pk2[:, 5 * d:5 * d + 5], T.tr2[:, d:160:32])
+    V.wait_ge(S.ac, npk)
+    for a in range(4):
+        n2 = ts(T.l2[32 * a:32 * a + 32, 0:25], T.pk2[:], 200.0, op.add)
+
+    lo = float(COLS * me)
+    V.wait_ge(S.d_e3, 16)
+    V.wait_ge(S.gs, more)
+    na = ts(T.a3[R, :], T.e3[R, :], lo, op.is_ge)
+    ts(T.b3[R, :], T.e3[R, :], lo + COLS, op.is_ge)
+    nc = v("scan", T.c3[R, :], T.a3[R, :], T.b3[R, :], 0.0, op.add, op.subtract)
+    A.wait_ge(S.v, na)
+    A.wait_ge(S.gs, more)
+    act(T.nb3[R, :], T.a3[R, :], COPY, accum_out=T.na3[R, :])
+    act(T.lb3[R, :], T.sam[R, :], COPY, scale=T.na3[R, 0:1])
+    A.wait_ge(S.v, nc)
+    nl = act(T.la3[R, :], T.lsa[R, :], COPY, scale=T.c3[R, W - 1:W])
+    V.wait_ge(S.d_t3, 128)
+    v("cp", T.tq3[:, 0:32], T.t3[:])
+    v("tr", T.tq3[:, 32:64], T.tq3[:, 0:32])
+    v("cp", T.of3[:], T.tq3[:, 32:56])
+    V.wait_ge(S.ac, nl)
+    tt(T.lc3[R, 0:30], T.la3[R, :], T.lb3[R, :], op.subtract)
+    v("tr", T.lt3[:], T.lc3[:])
+    v("red", T.bs3[:], T.lt3[:], X, op.add)
+
+    def rest1():
+        ts(T.g3[R, :], T.c3[R, :], T.bs3[R, 0:1], op.add)
+        ts(T.pp3[R, :], T.g3[R, :], 0.2, op.mult, 76.2, op.add)
+        ts(T.k3[R, :], T.pp3[R, :], -5.0, op.mult, 383.0, op.add)
+        tt(T.k3[R, :], T.k3[R, :], T.g3[R, :], op.add)
+        V.wait_ge(S.ac, nc3)
+        tt(T.cn3[:], T.cr3[:, :, 5:10], T.cr3[:, :, 0:5], op.subtract)
+        v("scan", T.in3[:], T.rst[:], T.cn3[:], 0.0, op.mult, op.add)
+        tt(T.x3[:], T.in3[:], T.cr3[:, :, 5:10], op.subtract)
+        tt(T.in3[:], T.x3[:], T.kk8[:], op.add)
+        tt(T.x3[:], T.in3[:], T.ms3[:], op.mult)
+        tt(T.xs3[:, 0:5], T.x3[:, 0:25:5], T.x3[:, 1:25:5], op.add)
+        tt(T.xs3[:, 5:10], T.x3[:, 2:25:5], T.x3[:, 3:25:5], op.add)
+        tt(T.xt3[:], T.xs3[:, 0:5], T.xs3[:, 5:10], op.add)
+        tt(T.xs3[:, 0:5], T.xt3[:], T.x3[:, 4:25:5], op.add)
+
+    def rest2():
+        for k in range(N):
+            ts(T.sg3[R, W * k:W * k + W], T.k3[R, :], float(k), op.is_equal, T.xs3[R, k:k + 1], op.mult)
+        tt(T.sa3[R, :], T.sg3[R, 0:2 * W], T.sg3[R, 2 * W:4 * W], op.add)
+        tt(T.sb3[R, :], T.sa3[R, 0:W], T.sa3[R, W:2 * W], op.add)
+        tt(T.g3[R, :], T.sb3[R, :], T.sg3[R, 4 * W:5 * W], op.add)
+        nv3 = tt(T.v3[R, :], T.g3[R, :], T.pp3[R, :], op.add)
+        g.sync.wait_ge(S.v, nv3)
+        g.sync.dma_start(T.val3[0:80:16, :], T.v3[R, :]).then_inc(S.d_v3, 16)
+
+    V.wait_ge(S.s1c, landed)
+    V.wait_ge(S.d_o1, 32)
+    k2 = v("cp", T.q3[:].bitcast(dt.uint32), T.ql[:].bitcast(dt.uint32).indirect(T.l2[:, 0:25]))
+    A.wait_ge(S.v, n2)
+    A.wait_ge(S.s1p, landed)
+    A.wait_ge(S.d_o1, 32)
+    A.activation(T.p3[:], T.pl[:].indirect(T.l2[:, 0:25]), COPY).then_inc(S.ap, 1)
+    g.wait_ge(S.v, k2)
+    spread(lambda r: T.q3[:, cut(r, SLOT)].bitcast(dt.uint8), T.qm[:, cut(me, SLOT)].bitcast(dt.uint8), S.s2c)
+    g.wait_ge(S.ap, 2)
+    spread(lambda r: T.p3[:, cut(r, SLOT)], T.pm[:, cut(me, SLOT)], S.s2p)
+    g.sync.wait_ge(S.v, k2)
+    g.sync.dma_start(T.qm[:, cut(me, SLOT)].bitcast(dt.uint8), T.q3[:, cut(me, SLOT)].bitcast(dt.uint8)).then_inc(S.d_o2, 16)
+    g.sync.wait_ge(S.ap, 2)
+    g.sync.dma_start(T.pm[:, cut(me, SLOT)], T.p3[:, cut(me, SLOT)]).then_inc(S.d_o2, 16)
+
+    rest1()
+    rest2()
+    V.wait_ge(S.d_w, 16)
+    v("qz", T.wq[:], T.wp[:], T.wt[:])
+    V.wait_ge(S.d_v3, 16)
+    v("cp", T.win3[:].indirect(T.of3[:]), T.val3[:])
+    mine = T.win3[:, COLS * me:COLS * me + COLS]
+    v("cp", T.dup3[:, :, 0:16], mine)
+    v("cp", T.dup3[:, :, 16:32], mine)
+    v("tr", T.tr3[:], T.dup3[:])
+    tt(T.sm3[:], T.tr3[:, 0:768:32], T.tr3[:, 16:768:32], op.add)
+    v("cp", T.su3[:, 0:24], T.sm3[32:64, :])
+    v("cp", T.su3[:, 24:48], T.sm3[64:96, :])
+    tt(T.su3[:, 48:72], T.sm3[0:32, :], T.su3[:, 0:24], op.add)
+    tt(T.su3[:, 48:72], T.su3[:, 48:72], T.su3[:, 24:48], op.add)
+    for a in range(4):
+        n3 = ts(T.l3[32 * a:32 * a + 32, :], T.su3[:, 48:72], 200.0, op.add)
+
+    V.wait_ge(S.s2c, landed)
+    V.wait_ge(S.d_o2, 32)
+    A.wait_ge(S.v, n3)
+    A.wait_ge(S.s2p, landed)
+    A.wait_ge(S.d_o2, 32)
+    HALF = COLS // 2
+    for h in range(2):
+        c = slice(HALF * h, HALF * h + HALF)
+        off = T.l3[:, 12 * h:12 * h + 12]
+        nk = v("cp", T.q4[:, c].bitcast(dt.uint32), T.qm[:].bitcast(dt.uint32).indirect(off))
+        A.activation(T.p4[:, c], T.pm[:].indirect(off), COPY).then_inc(S.ap, 1)
+        g.tensor.wait_ge(S.v, nk)
+        g.tensor.wait_ge(S.ap, 3 + h)
+        for o in range(2):
+            b = 2 * h + o
+            g.tensor.matmul_mx(T.ps[:, 512 * b:512 * b + HALF], T.wq[:, 128 * o:128 * o + 128], T.wp[:, 128 * o:128 * o + 128],
+                               T.q4[:, c], T.p4[:, c], True, True).then_inc(S["m%d" % b], 1)
+    for h in range(2):
+        for o in range(2):
+            b = 2 * h + o
+            y = T.ys[:, COLS * o + HALF * h:COLS * o + HALF * h + HALF]
+            out = T.y[:, COLS * o + HALF * h:COLS * o + HALF * h + HALF]
+            if o == 0:
+                V.wait_ge(S["m%d" % b], 1)
+                ny = v("cp", y, T.ps[:, 512 * b:512 * b + HALF])
+                g.sync.wait_ge(S.v, ny)
+                g.sync.dma_start(out, y).then_inc(S.st, 16)
+            else:
+                A.wait_ge(S["m%d" % b], 1)
+                act(y, T.ps[:, 512 * b:512 * b + HALF], COPY)
+                A.wait_ge(S.ac, cnt["ac"])
+                A.dma_start(out, y).then_inc(S.st2, 16)
+    g.sync.wait_ge(S.st, 32)
+    A.wait_ge(S.st2, 32)
+    g.wait_ge(S.v, cnt["v"])
+    g.wait_ge(S.loc, 5 * landed)

@@ -13,23 +13,23 @@ X4, U8 = "float8_e4m3fn_x4", "uint8"
 SMALL = {
     X4: "q:128,384 wq:128,256 q2:128,400 ql:128,400 q3:128,400 qm:128,400 q4:128,384",
     U8: "p:128,384 wp:128,256 p2:128,400 pl:128,400 p3:128,400 pm:128,400 p4:128,384",
-    BF: "xt:128,1536 wt:128,1024 val1:128,192 win1:128,400 dup1:128,25,32 tr1:128,800 dup2:32,5,32 tr2:32,160 v3:32,64 "
-        "val3:128,384 win3:128,1920 dup3:128,24,32 tr3:128,768",
-    I32: "qf:128,192 e1:32,64 pp1:32,12 e2:32,384 ci2:32,30 e3:32,64 pp3:32,64 t3:128,32",
+    BF: "xt:128,1536 wt:128,1024 val1:128,192 win1:128,400 dup1:128,25,32 tr1:128,800 v3:32,64 val3:128,384 win3:128,1920 "
+        "dup3:128,24,32 tr3:128,768",
+    I32: "qf:128,192 e1:32,64 e2:32,384 ci2:128,30 e3:32,64 pp3:32,64 t3:128,32",
     U16: "of1:128,12 l1:128,26 l2:128,26 of3:128,24 l3:128,24",
-    F32: "ys:128,768 cst:128,160 ct:128,160 fr:128,192 lm:32,32 tf:128,192 uf:128,192 ones:32,64 rst:32,25 ms2:32,50 tcon:32,80 "
-         "sam:32,30 lsa:32,30 ms3:32,25 kk8:32,25 a1:32,64 b1:32,64 i1:32,64 c1:32,64 g1:32,64 z1:32,64 zt1:32,64 ln1:32,32 "
-         "lt1:32,32 bs1:32,1 s1a:32,52 s1b:32,38 s1:32,12 y1:32,12 sm1:128,25 cm2:32,384 sg2:32,1 bm2:32,32 row2:32,32 "
-         "cn2:32,25 m2:32,50 sh2:32,25 mm2:32,50 ta2:32,40 tb2:32,35 tc2:32,30 seg:32,400 sa2:32,160 sb2:32,80 pk2:32,25 a3:32,64 "
-         "b3:32,64 c3:32,64 na3:32,1 nb3:32,64 la3:32,30 lb3:32,30 lc3:32,32 lt3:32,32 bs3:32,1 g3:32,64 k3:32,64 cx3:32,5,10 "
-         "cr3:32,5,10 cn3:32,25 in3:32,25 x3:32,25 xt3:32,5 xs3:32,10 sg3:32,320 sa3:32,128 sb3:32,64 tq3:128,64 sm3:128,24 "
-         "su3:32,72",
+    F32: "ys:128,768 cst:128,224 ct:128,224 fr:128,192 lm:32,32 tf:128,192 uf:128,192 ones:128,64 rst:128,25 tc0:128,5 tcw:128,5 "
+         "sa0:32,30 sam:32,30 lsa:32,30 ms0:32,25 ms3:32,25 a1:32,64 b1:32,64 i1:32,64 c1:32,64 g1:32,64 z1:32,64 zt1:32,64 "
+         "ln1:32,32 lt1:32,32 bs1:32,1 s1a:32,52 s1b:32,38 s1:32,12 sm1:128,25 cm2:32,384 sg2:32,1 bm2:32,32 row2:128,32 "
+         "cn2:128,25 cu2:128,25 sh2:128,25 de2:128,25 seg:128,125 sa2:128,50 sb2:128,25 sc2:128,25 a3:32,64 b3:32,64 c3:32,64 "
+         "na3:32,1 la3:32,30 lb3:32,30 lc3:32,32 lt3:32,32 bs3:32,1 g3:32,64 h3:32,64 k3:32,64 pk3:32,64 pl3:32,64 cx3:32,5,10 "
+         "cr3:32,5,10 cn3:32,25 in3:32,25 x3:32,25 xm3:32,25 xs3:32,10 xt3:32,5 xu3:32,5 sg3:32,320 sa3:32,128 sb3:32,64 sc3:32,64 "
+         "tq3:128,32 tr0:128,32 sm3:128,24 su3:32,96",
 }
 SCRATCH = {"ps": ("psum", [128, 2048], F32), "lists": ("dram", [N, 128, 3], I32)}
 for _t in SMALL:
     for _b in SMALL[_t].split():
         SCRATCH[_b.split(":")[0]] = ("sbuf", [int(_n) for _n in _b.split(":")[1].split(",")], _t)
-SEMAPHORES = ["v", "gs", "d_e1", "d_x", "d_w", "d_l", "d_e2", "d_e3", "d_t3", "d_o1", "d_v3", "d_o2",
+SEMAPHORES = ["v", "w", "ga", "gb", "gd", "d_e1", "d_x", "d_w", "d_l", "d_e2", "d_e3", "d_t3", "d_o1", "d_v3", "d_o2",
               "sl", "s1c", "s1p", "s2c", "s2p", "loc", "ap", "m0", "m1", "m2", "m3", "ac", "st", "st2"]
 
 
@@ -41,42 +41,40 @@ def rank_program(g, core, T, topo):
     op = AluOpType
     X, COPY, LINE = AxisListType.X, ActivationFunctionType.Copy, ActivationFunctionType.Identity
     others = [r for r in range(N) if r != me]
-    cnt = {"v": 0, "gs": 0, "ac": 0}
+    cnt = {"v": 0, "w": 0, "ac": 0, "ga": 0, "gb": 0, "gd": 0}
+    CALL = {"ts": V.tensor_scalar, "tt": V.tensor_tensor, "cp": V.tensor_copy, "ms": V.memset, "red": V.tensor_reduce,
+            "scan": V.tensor_tensor_scan, "tr": V.transpose, "qz": V.quantize_mx}
 
-    def v(name, *args):
-        if cnt["v"]:
-            V.wait_ge(S.v, cnt["v"])
-        calls = {"ts": V.tensor_scalar, "tt": V.tensor_tensor, "cp": V.tensor_copy, "ms": V.memset, "red": V.tensor_reduce,
-                 "scan": V.tensor_tensor_scan, "tr": V.transpose, "qz": V.quantize_mx}
-        calls[name](*args).then_inc(S.v, 1)
-        cnt["v"] += 1
-        return cnt["v"]
+    def vec(line, free, name, args):
+        if cnt[line] and not free:
+            V.wait_ge(S[line], cnt[line])
+        if name == "ts":
+            out, a, s1, o1 = args[:4]
+            args = (out, a, s1, None, o1) if len(args) == 4 else (out, a, s1, args[4], o1, args[5])
+        CALL[name](*args).then_inc(S[line], 1)
+        cnt[line] += 1
+        return cnt[line]
+    v = lambda name, *args: vec("v", False, name, args)
+    vf = lambda name, *args: vec("v", True, name, args)
+    w = lambda name, *args: vec("w", False, name, args)
+    wf = lambda name, *args: vec("w", True, name, args)
 
-    def ts(out, a, s1, o1, s2=None, o2=None):
-        return v("ts", out, a, s1, s2, o1) if o2 is None else v("ts", out, a, s1, s2, o1, o2)
-
-    def tt(out, a, b, o):
-        return v("tt", out, a, b, o)
-
-    def act(out, in_, func, **k):
-        if cnt["ac"]:
+    def act(free, out, in_, func, **k):
+        if cnt["ac"] and not free:
             A.wait_ge(S.ac, cnt["ac"])
         A.activation(out, in_, func, **k).then_inc(S.ac, 1)
         cnt["ac"] += 1
         return cnt["ac"]
 
-    def gc(call, *args, **k):
-        if cnt["gs"]:
-            g.wait_ge(S.gs, cnt["gs"])
-        call(*args, **k).then_inc(S.gs, 1)
-        cnt["gs"] += 1
-        return cnt["gs"]
+    def iota(line, out, pattern, base=0, cm=0):
+        g.iota(out, pattern, base, cm, allow_small_or_imprecise_dtypes=True).then_inc(S[line], 1)
+        cnt[line] += 1
 
-    def iota(out, pattern, base=0, cm=0):
-        return gc(g.iota, out, pattern, base, cm, allow_small_or_imprecise_dtypes=True)
-
-    def sel(out, in_, pattern, how, base, cm):
-        return gc(g.affine_select, out, in_, pattern, how, 0.0, base, cm)
+    def sel(line, free, out, in_, pattern, how, base, cm):
+        if not free:
+            g.wait_ge(S[line], cnt[line])
+        g.affine_select(out, in_, pattern, how, 0.0, base, cm).then_inc(S[line], 1)
+        cnt[line] += 1
 
     for d in range(N):
         (g.sync if d % 2 else A).dma_start(T.e1[H * d:H * d + H, :], T.to[:]).then_inc(S.d_e1, 16)
@@ -85,26 +83,29 @@ def rank_program(g, core, T, topo):
     A.dma_start(T.xt[:, 768:1536], T.x[:, 768:1536]).then_inc(S.d_x, 16)
     g.sync.dma_start(T.wt[:], T.w[:]).then_inc(S.d_w, 16)
 
-    v("ms", T.cst[:], 0.0)
+    z0 = vf("ms", T.cst[:], 0.0)
     v("ms", T.z1[:], 0.0)
-    v("ms", T.ln1[:], 0.0)
-    v("ms", T.win1[:], 0.0)
-    g.wait_ge(S.v, 1)
-    iota(T.cst[0:32, 32:62], [[COLS, N], [0, H]])
-    iota(T.cst[0:32, 64:94], [[COLS, N], [0, H]], COLS)
-    iota(T.cst[0:32, 96:126], [[COLS, N + 1], [0, N]])
-    iota(T.cst[0:32, 128:158], [[0, N + 1], [5 * SLOT, N]])
-    rows = iota(T.cst[:, 0:32], [[32, 2], [0, 16]])
-    order = iota(T.fr[:], [[64, 2], [2 * W, H], [2, 16]], -23)
-    iota(T.ones[:], [[0, 64]], 1)
-    tri = sel(T.lm[:], T.ones[:, 0:32], [[1, 32]], op.is_gt, 0, -1)
-    V.wait_ge(S.gs, rows)
-    v("tr", T.ct[:], T.cst[:])
-    V.wait_ge(S.gs, order)
-    ts(T.qf[:], T.fr[:], T.ct[:, 0:1], op.add, 1.0 / 48, op.mult)
-    ts(T.tf[:], T.fr[:], T.ct[:, 0:1], op.add, 8.0, op.mult)
-    ts(T.uf[:], T.qf[:], -383.0, op.mult, -8.0, op.add)
-    tt(T.val1[:], T.tf[:], T.uf[:], op.add)
+    vf("ms", T.ln1[:], 0.0)
+    vf("ms", T.win1[:], 0.0)
+    g.wait_ge(S.v, z0)
+    iota("ga", T.cst[0:32, 32:62], [[COLS, N], [0, H]])
+    iota("ga", T.cst[0:32, 64:94], [[COLS, N], [0, H]], COLS)
+    iota("ga", T.cst[:, 0:32], [[32, 2], [0, 16]])
+    iota("ga", T.cst[0:32, 96:126], [[COLS, N + 1], [0, N]])
+    iota("ga", T.cst[0:32, 128:158], [[0, N + 1], [5 * SLOT, N]])
+    iota("ga", T.cst[0:32, 160:190], [[SLOT, N], [0, H]], WHOLE - 200)
+    iota("ga", T.cst[:, 192:224], [[0, 2], [1, 16]])
+    iota("gb", T.ones[:], [[0, 64]], 1)
+    iota("gb", T.fr[:], [[64, 2], [2 * W, H], [2, 16]], -23)
+    sel("gb", False, T.lm[:], T.ones[0:32, 0:32], [[1, 32]], op.is_gt, 0, -1)
+    V.wait_ge(S.ga, cnt["ga"])
+    nct = v("tr", T.ct[:], T.cst[:])
+    V.wait_ge(S.gb, cnt["gb"])
+    V.wait_ge(S.v, nct)
+    wf("ts", T.qf[:], T.fr[:], T.ct[:, 0:1], op.add, 1.0 / 48, op.mult)
+    wf("ts", T.tf[:], T.fr[:], T.ct[:, 0:1], op.add, 8.0, op.mult)
+    w("ts", T.uf[:], T.qf[:], -383.0, op.mult, -8.0, op.add)
+    w("tt", T.val1[:], T.tf[:], T.uf[:], op.add)
 
     per = len(topo.engines(core, T.cores[others[0]])) // len(others)
     landed = per * len(others)
@@ -120,53 +121,64 @@ def rank_program(g, core, T, topo):
     g.wait_ge(S.d_l, 16)
     spread(lambda r: T.lists[me], T.lists[me], S.sl)
 
-    t0 = iota(T.t3[:], [[0, 32]])
-    iota(T.bm2[:], [[0, 32]])
-    sel(T.rst[:], T.ones[:, 0:25], [[0, 5], [1, 5]], op.is_gt, 0, 0)
-    sel(T.ms2[:], T.ones[:, 0:50], [[0, 2], [1, 5], [0, 5]], op.is_equal, 0, -1)
-    tables = iota(T.tcon[:], [[1, SLOT]])
-    iota(T.lc3[:], [[0, 32]])
-    sel(T.lb3[:], T.ones[:, 0:30], [[-H, 5], [0, H]], op.is_ge, 0, 1)
-    sel(T.sam[:], T.lb3[:], [[H, 5], [0, H]], op.is_ge, H - 1, -1)
-    sel(T.lsa[:], T.sam[:], [[1, 30]], op.is_gt, 0, -1)
-    sel(T.cn3[:], T.ones[:, 0:25], [[0, 5], [-H, 5]], op.is_ge, 0, 1)
-    sel(T.ms3[:], T.cn3[:], [[0, 5], [H, 5]], op.is_ge, H - 1, -1)
-    iota(T.kk8[:], [[SLOT, 5], [SLOT, 5]], WHOLE - 200)
-    iota(T.val3[:], [[0, COLS]])
-    more = iota(T.win3[:, COLS * me:COLS * me + COLS], [[0, COLS]])
+    iota("gd", T.t3[:], [[0, 32]])
+    iota("gd", T.bm2[:], [[0, 32]])
+    sel("gd", True, T.rst[:], T.ones[:, 0:25], [[0, 5], [1, 5]], op.is_gt, 0, 0)
+    iota("gd", T.tc0[:], [[16, 5]])
+    iota("gd", T.lc3[:], [[0, 32]])
+    sel("gd", True, T.sa0[:], T.ones[0:32, 0:30], [[-H, 5], [0, H]], op.is_ge, 0, 1)
+    sel("gd", True, T.ms0[:], T.ones[0:32, 0:25], [[0, 5], [-H, 5]], op.is_ge, 0, 1)
+    sel("gd", False, T.sam[:], T.sa0[:], [[H, 5], [0, H]], op.is_ge, H - 1, -1)
+    sel("gd", True, T.ms3[:], T.ms0[:], [[0, 5], [H, 5]], op.is_ge, H - 1, -1)
+    sel("gd", False, T.lsa[:], T.sam[:], [[1, 30]], op.is_gt, 0, -1)
+    iota("gd", T.val3[:], [[0, COLS]])
+    iota("gd", T.win3[:, COLS * me:COLS * me + COLS], [[0, COLS]])
 
     R = slice(0, 30)
     V.wait_ge(S.d_e1, 80)
-    ts(T.a1[R, :], T.e1[R, :], T.ct[R, 32:33], op.is_ge)
-    ts(T.b1[R, :], T.e1[R, :], T.ct[R, 64:65], op.is_ge)
+    vf("ts", T.a1[R, :], T.e1[R, :], T.ct[R, 32:33], op.is_ge)
+    vf("ts", T.b1[R, :], T.e1[R, :], T.ct[R, 64:65], op.is_ge)
     v("scan", T.c1[R, :], T.a1[R, :], T.b1[R, :], 0.0, op.add, op.subtract)
-    V.wait_ge(S.gs, tri)
-    ts(T.ln1[R, :], T.lm[R, :], T.c1[R, W - 1:W], op.mult)
+    v("ts", T.ln1[R, :], T.lm[R, :], T.c1[R, W - 1:W], op.mult)
+    wf("tt", T.i1[R, :], T.a1[R, :], T.b1[R, :], op.subtract)
     v("tr", T.lt1[:], T.ln1[:])
     v("red", T.bs1[:], T.lt1[:], X, op.add)
-    tt(T.i1[R, :], T.a1[R, :], T.b1[R, :], op.subtract)
-    ts(T.g1[R, :], T.c1[R, :], T.bs1[R, 0:1], op.add, float(SLOT), op.mult)
-    tt(T.z1[R, :], T.g1[R, :], T.i1[R, :], op.mult)
+    v("ts", T.g1[R, :], T.c1[R, :], T.bs1[R, 0:1], op.add)
+    V.wait_ge(S.w, cnt["w"])
+    v("tt", T.z1[R, :], T.g1[R, :], T.i1[R, :], op.mult)
     v("tr", T.zt1[:], T.z1[:])
-    tt(T.s1a[:], T.zt1[:, 0:52], T.zt1[:, 12:64], op.add)
-    tt(T.s1b[:], T.s1a[:, 0:38], T.s1a[:, 6:44], op.add)
-    tt(T.s1[:, 0:6], T.s1b[:, 0:6], T.zt1[:, 24:30], op.add)
-    tt(T.s1[:, 6:12], T.s1b[:, 32:38], T.zt1[:, 56:62], op.add)
-    ts(T.pp1[:], T.s1[:], 0.2 / SLOT, op.mult, -0.6, op.add)
-    ts(T.y1[:], T.pp1[:], float(1 - 5 * SLOT), op.mult, -float(SLOT), op.add)
-    tt(T.s1[:], T.s1[:], T.y1[:], op.add)
-    for a in range(4):
-        v("cp", T.of1[32 * a:32 * a + 32, :], T.s1[:])
-    v("cp", T.win1[:, 0:400].indirect(T.of1[:, 0:12]), T.val1[:])
-    v("cp", T.dup1[:, :, 0:16], T.win1[:])
-    v("cp", T.dup1[:, :, 16:32], T.win1[:])
-    v("tr", T.tr1[:], T.dup1[:])
-    tt(T.sm1[:], T.tr1[:, 0:800:32], T.tr1[:, 16:800:32], op.add)
-    ts(T.l1[:, 0:25], T.sm1[:], 192.0, op.add)
+
+    def pack(b):
+        return wf("qz", T.q[:, 128 * b:128 * b + 128], T.p[:, 128 * b:128 * b + 128], T.xt[:, 512 * b:512 * b + 512])
+    v("tt", T.s1a[:], T.zt1[:, 0:52], T.zt1[:, 12:64], op.add)
     V.wait_ge(S.d_x, 32)
-    n1 = v("qz", T.q[:], T.p[:], T.xt[:])
+    pack(0)
+    v("tt", T.s1b[:], T.s1a[:, 0:38], T.s1a[:, 6:44], op.add)
+    pack(1)
+    v("tt", T.s1[:, 0:6], T.s1b[:, 0:6], T.zt1[:, 24:30], op.add)
+    vf("tt", T.s1[:, 6:12], T.s1b[:, 32:38], T.zt1[:, 56:62], op.add)
+    n1 = pack(2)
+    v("ts", T.of1[0:32, :], T.s1[:], -1.0, op.add)
+    for a in range(1, 4):
+        vf("ts", T.of1[32 * a:32 * a + 32, :], T.s1[:], -1.0, op.add)
+    nw1 = v("cp", T.win1[:, 0:400].indirect(T.of1[:, 0:12]), T.val1[:])
+    V.wait_ge(S.v, nw1)
+    A.wait_ge(S.v, nw1)
+    for k in range(N):
+        for u in (0, 16):
+            out, in_ = T.dup1[:, 5 * k:5 * k + 5, u:u + 16], T.win1[:, k:400:5]
+            if k < 3:
+                vf("cp", out, in_)
+            else:
+                nd1 = act(True, out, in_, COPY)
+    V.wait_ge(S.ac, nd1)
+    v("tr", T.tr1[:], T.dup1[:])
+    v("tt", T.sm1[:], T.tr1[:, 0:800:32], T.tr1[:, 16:800:32], op.add)
+    nl1 = v("ts", T.l1[:, 0:25], T.sm1[:], 192.0, op.add)
+    V.wait_ge(S.w, n1)
     k1 = v("cp", T.q2[:].bitcast(dt.uint32), T.q[:].bitcast(dt.uint32).indirect(T.l1[:, 0:25]))
-    A.wait_ge(S.v, n1)
+    A.wait_ge(S.w, n1)
+    A.wait_ge(S.v, nl1)
     A.activation(T.p2[:], T.p[:].indirect(T.l1[:, 0:25]), COPY).then_inc(S.ap, 1)
 
     cut = lambda r, n: slice(SLOT * r, SLOT * r + n)
@@ -180,7 +192,7 @@ def rank_program(g, core, T, topo):
     for d in range(N + 1):
         g.sync.dma_start(T.e2[N * d:N * d + N, :], T.lists[:]).then_inc(S.d_e2, 16)
     g.sync.dma_start(T.e3[R, :], T.lists[:]).then_inc(S.d_e3, 16)
-    g.sync.wait_ge(S.gs, t0)
+    g.sync.wait_ge(S.gd, cnt["gd"])
     for b in range(8):
         g.sync.dma_start(T.t3[32 * (b // 2):32 * (b // 2) + 24, 16 * (b % 2):16 * (b % 2) + 16], T.lists[b % N]).then_inc(S.d_t3, 16)
     g.sync.wait_ge(S.v, k1)
@@ -188,91 +200,113 @@ def rank_program(g, core, T, topo):
     g.sync.wait_ge(S.ap, 1)
     g.sync.dma_start(T.pl[:, cut(me, SLOT)], T.p2[:, cut(me, SLOT)]).then_inc(S.d_o1, 16)
 
-    V.wait_ge(S.d_e2, 96)
-    V.wait_ge(S.gs, tables)
-    ts(T.cm2[R, :], T.e2[R, :], T.ct[R, 96:97], op.is_ge)
-    v("red", T.sg2[R, :], T.cm2[R, :], X, op.add)
-    ts(T.bm2[R, :], T.ones[R, 0:32], T.sg2[R, 0:1], op.mult, T.ct[R, 128:129], op.subtract)
-    nrow = v("tr", T.row2[:], T.bm2[:])
-    ts(T.ci2[:], T.row2[:, 0:30], -0.2, op.mult, (386 - me) * 0.2, op.add)
-    tt(T.cn2[:], T.ci2[:, 5:30], T.ci2[:, 0:25], op.subtract)
-    v("scan", T.m2[:, 0:25], T.rst[:], T.cn2[:], 0.0, op.mult, op.add)
-    tt(T.sh2[:], T.ci2[:, 4:29], T.rst[:], op.mult)
-    tt(T.m2[:, 25:50], T.ci2[:, 0:25], T.sh2[:], op.subtract)
-    tt(T.mm2[:], T.m2[:], T.ms2[:], op.mult)
-    tt(T.ta2[:], T.mm2[:, 0:40], T.mm2[:, 10:50], op.add)
-    tt(T.tb2[:], T.ta2[:, 0:35], T.ta2[:, 5:40], op.add)
-    tt(T.tc2[:], T.tb2[:, 0:30], T.mm2[:, 20:50], op.add)
-    ts(T.seg[:, 0:SLOT], T.tcon[:], T.tc2[:, 25:26], op.add)
-    for r in range(1, N):
-        ts(T.seg[:, SLOT * r:SLOT * r + SLOT], T.tcon[:], T.tc2[:, r - 1:r], op.is_ge, T.tc2[:, 25 + r:26 + r], op.mult)
-    tt(T.sa2[:], T.seg[:, 0:160], T.seg[:, 160:320], op.add)
-    tt(T.sb2[:], T.sa2[:, 0:80], T.sa2[:, 80:160], op.add)
-    tt(T.sb2[:], T.sb2[:], T.seg[:, 320:400], op.add)
-    last = float(SLOT * (N - 1) + SENT1 - 1)
-    ts(T.dup2[:, :, 0:16], T.sb2[:], last, op.min, -200.0, op.add)
-    ts(T.dup2[:, :, 16:32], T.sb2[:], last, op.min, -200.0, op.add)
-    nt2 = v("tr", T.tr2[:], T.dup2[:])
+    lo = float(COLS * me)
+    mark = {}
 
+    def third():
+        V.wait_ge(S.d_e3, 16)
+        w("ts", T.a3[R, :], T.e3[R, :], lo, op.is_ge)
+        wf("ts", T.b3[R, :], T.e3[R, :], lo + COLS, op.is_ge)
+        yield
+        w("scan", T.c3[R, :], T.a3[R, :], T.b3[R, :], 0.0, op.add, op.subtract)
+        wf("red", T.na3[R, :], T.a3[R, :], X, op.add)
+        yield
+        w("ts", T.la3[R, :], T.lsa[R, :], T.c3[R, W - 1:W], op.mult)
+        wf("ts", T.lb3[R, :], T.sam[R, :], T.na3[R, 0:1], op.mult)
+        yield
+        w("tt", T.lc3[R, 0:30], T.la3[R, :], T.lb3[R, :], op.subtract)
+        V.wait_ge(S.d_t3, 128)
+        wf("cp", T.tq3[:], T.t3[:])
+        yield
+        w("tr", T.lt3[:], T.lc3[:])
+        wf("tr", T.tr0[:], T.tq3[:])
+        yield
+        w("red", T.bs3[:], T.lt3[:], X, op.add)
+        wf("cp", T.of3[:], T.tr0[:, 0:24])
+        yield
+        w("ts", T.g3[R, :], T.c3[R, :], T.bs3[R, 0:1], op.add)
+        V.wait_ge(S.ac, mark["nc3"])
+        wf("tt", T.cn3[:], T.cr3[:, :, 5:10], T.cr3[:, :, 0:5], op.subtract)
+        yield
+        w("ts", T.pp3[R, :], T.g3[R, :], 0.2, op.mult, 76.2, op.add)
+        wf("scan", T.in3[:], T.rst[0:32, :], T.cn3[:], 0.0, op.mult, op.add)
+        yield
+        w("ts", T.h3[R, :], T.pp3[R, :], -5.0, op.mult, 383.0, op.add)
+        wf("tt", T.x3[:], T.in3[:], T.cr3[:, :, 5:10], op.subtract)
+        yield
+        w("tt", T.k3[R, :], T.h3[R, :], T.g3[R, :], op.add)
+        wf("tt", T.xm3[:], T.x3[:], T.ms3[:], op.mult)
+        yield
+        w("ts", T.pk3[R, :], T.k3[R, :], float(SLOT), op.mult, T.ct[R, 160:161], op.add)
+        wf("tt", T.xs3[:, 0:5], T.xm3[:, 0:25:5], T.xm3[:, 1:25:5], op.add)
+        wf("tt", T.xs3[:, 5:10], T.xm3[:, 2:25:5], T.xm3[:, 3:25:5], op.add)
+        yield
+        w("tt", T.xt3[:], T.xs3[:, 0:5], T.xs3[:, 5:10], op.add)
+        wf("tt", T.pl3[R, :], T.pk3[R, :], T.pp3[R, :], op.add)
+        yield
+        w("tt", T.xu3[:], T.xt3[:], T.xm3[:, 4:25:5], op.add)
+        yield
+        w("ts", T.sg3[R, 0:W], T.k3[R, :], 0.0, op.is_equal, T.xu3[R, 0:1], op.mult)
+        for k in range(1, N):
+            wf("ts", T.sg3[R, W * k:W * k + W], T.k3[R, :], float(k), op.is_equal, T.xu3[R, k:k + 1], op.mult)
+        yield
+        w("tt", T.sa3[R, :], T.sg3[R, 0:2 * W], T.sg3[R, 2 * W:4 * W], op.add)
+        wf("tt", T.sc3[R, :], T.sg3[R, 4 * W:5 * W], T.pl3[R, :], op.add)
+        yield
+        w("tt", T.sb3[R, :], T.sa3[R, 0:W], T.sa3[R, W:2 * W], op.add)
+        yield
+        mark["v3"] = w("tt", T.v3[R, :], T.sb3[R, :], T.sc3[R, :], op.add)
+    steps = third()
+
+    def step(n=1):
+        for _ in range(n):
+            if next(steps, 1) is not None:
+                return
+
+    V.wait_ge(S.gd, cnt["gd"])
+    wf("ts", T.tcw[:], T.tc0[:], T.ct[:, 192:193], op.add)
+    V.wait_ge(S.d_e2, 96)
+    v("ts", T.cm2[R, :], T.e2[R, :], T.ct[R, 96:97], op.is_ge)
+    step()
+    v("red", T.sg2[R, :], T.cm2[R, :], X, op.add)
+    step()
+    v("ts", T.bm2[R, :], T.ones[R, 0:32], T.sg2[R, 0:1], op.mult, T.ct[R, 128:129], op.subtract)
+    step()
+    nrow = v("tr", T.row2[0:32, :], T.bm2[:])
     A.wait_ge(S.v, nrow)
     for k in range(N):
-        act(T.cx3[:, k, :], T.row2[:, 5 * me:5 * me + 10], LINE, scale=-0.2, bias=(386 - k) * 0.2)
-    nc3 = act(T.cr3[:], T.cx3[:], LINE, bias=float(WHOLE))
-    A.wait_ge(S.v, nt2)
-    for d in (3, 4):
-        npk = act(T.pk2[:, 5 * d:5 * d + 5], T.tr2[:, d:160:32], COPY)
-    for d in range(3):
-        v("cp", T.pk2[:, 5 * d:5 * d + 5], T.tr2[:, d:160:32])
-    V.wait_ge(S.ac, npk)
-    for a in range(4):
-        n2 = ts(T.l2[32 * a:32 * a + 32, 0:25], T.pk2[:], 200.0, op.add)
-
-    lo = float(COLS * me)
-    V.wait_ge(S.d_e3, 16)
-    V.wait_ge(S.gs, more)
-    na = ts(T.a3[R, :], T.e3[R, :], lo, op.is_ge)
-    ts(T.b3[R, :], T.e3[R, :], lo + COLS, op.is_ge)
-    nc = v("scan", T.c3[R, :], T.a3[R, :], T.b3[R, :], 0.0, op.add, op.subtract)
-    A.wait_ge(S.v, na)
-    A.wait_ge(S.gs, more)
-    act(T.nb3[R, :], T.a3[R, :], COPY, accum_out=T.na3[R, :])
-    act(T.lb3[R, :], T.sam[R, :], COPY, scale=T.na3[R, 0:1])
-    A.wait_ge(S.v, nc)
-    nl = act(T.la3[R, :], T.lsa[R, :], COPY, scale=T.c3[R, W - 1:W])
-    V.wait_ge(S.d_t3, 128)
-    v("cp", T.tq3[:, 0:32], T.t3[:])
-    v("tr", T.tq3[:, 32:64], T.tq3[:, 0:32])
-    v("cp", T.of3[:], T.tq3[:, 32:56])
-    V.wait_ge(S.ac, nl)
-    tt(T.lc3[R, 0:30], T.la3[R, :], T.lb3[R, :], op.subtract)
-    v("tr", T.lt3[:], T.lc3[:])
-    v("red", T.bs3[:], T.lt3[:], X, op.add)
-
-    def rest1():
-        ts(T.g3[R, :], T.c3[R, :], T.bs3[R, 0:1], op.add)
-        ts(T.pp3[R, :], T.g3[R, :], 0.2, op.mult, 76.2, op.add)
-        ts(T.k3[R, :], T.pp3[R, :], -5.0, op.mult, 383.0, op.add)
-        tt(T.k3[R, :], T.k3[R, :], T.g3[R, :], op.add)
-        V.wait_ge(S.ac, nc3)
-        tt(T.cn3[:], T.cr3[:, :, 5:10], T.cr3[:, :, 0:5], op.subtract)
-        v("scan", T.in3[:], T.rst[:], T.cn3[:], 0.0, op.mult, op.add)
-        tt(T.x3[:], T.in3[:], T.cr3[:, :, 5:10], op.subtract)
-        tt(T.in3[:], T.x3[:], T.kk8[:], op.add)
-        tt(T.x3[:], T.in3[:], T.ms3[:], op.mult)
-        tt(T.xs3[:, 0:5], T.x3[:, 0:25:5], T.x3[:, 1:25:5], op.add)
-        tt(T.xs3[:, 5:10], T.x3[:, 2:25:5], T.x3[:, 3:25:5], op.add)
-        tt(T.xt3[:], T.xs3[:, 0:5], T.xs3[:, 5:10], op.add)
-        tt(T.xs3[:, 0:5], T.xt3[:], T.x3[:, 4:25:5], op.add)
-
-    def rest2():
-        for k in range(N):
-            ts(T.sg3[R, W * k:W * k + W], T.k3[R, :], float(k), op.is_equal, T.xs3[R, k:k + 1], op.mult)
-        tt(T.sa3[R, :], T.sg3[R, 0:2 * W], T.sg3[R, 2 * W:4 * W], op.add)
-        tt(T.sb3[R, :], T.sa3[R, 0:W], T.sa3[R, W:2 * W], op.add)
-        tt(T.g3[R, :], T.sb3[R, :], T.sg3[R, 4 * W:5 * W], op.add)
-        nv3 = tt(T.v3[R, :], T.g3[R, :], T.pp3[R, :], op.add)
-        g.sync.wait_ge(S.v, nv3)
-        g.sync.dma_start(T.val3[0:80:16, :], T.v3[R, :]).then_inc(S.d_v3, 16)
+        act(True, T.cx3[:, k, :], T.row2[0:32, 5 * me:5 * me + 10], LINE, scale=-0.2, bias=(386 - k) * 0.2)
+    mark["nc3"] = act(False, T.cr3[:], T.cx3[:], LINE, bias=float(WHOLE))
+    step()
+    v("cp", T.row2[32:64, :], T.row2[0:32, :])
+    vf("cp", T.row2[64:96, :], T.row2[0:32, :])
+    vf("cp", T.row2[96:128, :], T.row2[0:32, :])
+    v("ts", T.ci2[:], T.row2[:, 0:30], -0.2, op.mult, (386 - me) * 0.2, op.add)
+    step()
+    v("tt", T.cn2[:], T.ci2[:, 5:30], T.ci2[:, 0:25], op.subtract)
+    vf("tt", T.sh2[:], T.ci2[:, 4:29], T.rst[:], op.mult)
+    step()
+    v("scan", T.cu2[:], T.rst[:], T.cn2[:], 0.0, op.mult, op.add)
+    nde = vf("tt", T.de2[:], T.ci2[:, 0:25], T.sh2[:], op.subtract)
+    step()
+    V.wait_ge(S.v, nde)
+    A.wait_ge(S.v, nde)
+    for r in range(N):
+        for d in range(N):
+            out, e = T.seg[:, 25 * r + 5 * d:25 * r + 5 * d + 5], T.de2[:, 5 * d + r:5 * d + r + 1]
+            if r == 0:
+                nsg = act(d > 0, out, T.tcw[:], LINE, bias=e)
+            else:
+                vf("ts", out, T.tcw[:], T.cu2[:, 5 * d + r - 1:5 * d + r], op.is_ge, e, op.mult)
+    step()
+    V.wait_ge(S.ac, nsg)
+    v("tt", T.sa2[:], T.seg[:, 0:50], T.seg[:, 50:100], op.add)
+    step()
+    v("tt", T.sb2[:], T.sa2[:, 0:25], T.sa2[:, 25:50], op.add)
+    step()
+    v("tt", T.sc2[:], T.sb2[:], T.seg[:, 100:125], op.add)
+    step()
+    n2 = v("ts", T.l2[:, 0:25], T.sc2[:], float(SLOT * (N - 1) + SENT1 - 1), op.min)
 
     V.wait_ge(S.s1c, landed)
     V.wait_ge(S.d_o1, 32)
@@ -290,27 +324,30 @@ def rank_program(g, core, T, topo):
     g.sync.wait_ge(S.ap, 2)
     g.sync.dma_start(T.pm[:, cut(me, SLOT)], T.p3[:, cut(me, SLOT)]).then_inc(S.d_o2, 16)
 
-    rest1()
-    rest2()
+    step(99)
+    g.sync.wait_ge(S.w, mark["v3"])
+    g.sync.dma_start(T.val3[0:80:16, :], T.v3[R, :]).then_inc(S.d_v3, 16)
     V.wait_ge(S.d_w, 16)
-    v("qz", T.wq[:], T.wp[:], T.wt[:])
+    w("qz", T.wq[:], T.wp[:], T.wt[:])
     V.wait_ge(S.d_v3, 16)
-    v("cp", T.win3[:].indirect(T.of3[:]), T.val3[:])
+    w("cp", T.win3[:].indirect(T.of3[:]), T.val3[:])
     mine = T.win3[:, COLS * me:COLS * me + COLS]
-    v("cp", T.dup3[:, :, 0:16], mine)
-    v("cp", T.dup3[:, :, 16:32], mine)
-    v("tr", T.tr3[:], T.dup3[:])
-    tt(T.sm3[:], T.tr3[:, 0:768:32], T.tr3[:, 16:768:32], op.add)
-    v("cp", T.su3[:, 0:24], T.sm3[32:64, :])
-    v("cp", T.su3[:, 24:48], T.sm3[64:96, :])
-    tt(T.su3[:, 48:72], T.sm3[0:32, :], T.su3[:, 0:24], op.add)
-    tt(T.su3[:, 48:72], T.su3[:, 48:72], T.su3[:, 24:48], op.add)
-    for a in range(4):
-        n3 = ts(T.l3[32 * a:32 * a + 32, :], T.su3[:, 48:72], 200.0, op.add)
+    w("cp", T.dup3[:, :, 0:16], mine)
+    wf("cp", T.dup3[:, :, 16:32], mine)
+    w("tr", T.tr3[:], T.dup3[:])
+    w("tt", T.sm3[:], T.tr3[:, 0:768:32], T.tr3[:, 16:768:32], op.add)
+    w("cp", T.su3[:, 0:24], T.sm3[32:64, :])
+    wf("cp", T.su3[:, 24:48], T.sm3[64:96, :])
+    w("tt", T.su3[:, 48:72], T.sm3[0:32, :], T.su3[:, 0:24], op.add)
+    w("tt", T.su3[:, 72:96], T.su3[:, 48:72], T.su3[:, 24:48], op.add)
+    w("ts", T.l3[0:32, :], T.su3[:, 72:96], 200.0, op.add)
+    for a in range(1, 4):
+        n3 = wf("ts", T.l3[32 * a:32 * a + 32, :], T.su3[:, 72:96], 200.0, op.add)
 
     V.wait_ge(S.s2c, landed)
     V.wait_ge(S.d_o2, 32)
-    A.wait_ge(S.v, n3)
+    V.wait_ge(S.w, n3)
+    A.wait_ge(S.w, n3)
     A.wait_ge(S.s2p, landed)
     A.wait_ge(S.d_o2, 32)
     HALF = COLS // 2
@@ -337,7 +374,7 @@ def rank_program(g, core, T, topo):
                 g.sync.dma_start(out, y).then_inc(S.st, 16)
             else:
                 A.wait_ge(S["m%d" % b], 1)
-                act(y, T.ps[:, 512 * b:512 * b + HALF], COPY)
+                act(False, y, T.ps[:, 512 * b:512 * b + HALF], COPY)
                 A.wait_ge(S.ac, cnt["ac"])
                 A.dma_start(out, y).then_inc(S.st2, 16)
     g.sync.wait_ge(S.st, 32)

@@ -17,19 +17,19 @@ SMALL = {
         "dup3:128,24,32 tr3:128,768",
     I32: "qf:128,192 e1:32,64 e2:32,384 ci2:128,30 e3:32,64 pp3:32,64 t3:128,32",
     U16: "of1:128,12 l1:128,26 l2:128,26 of3:128,24 l3:128,24",
-    F32: "ys:128,768 cst:128,224 ct:128,224 fr:128,192 lm:32,32 tf:128,192 uf:128,192 ones:128,64 rst:128,25 tc0:128,5 tcw:128,5 "
-         "sa0:32,30 sam:32,30 lsa:32,30 ms0:32,25 ms3:32,25 a1:32,64 b1:32,64 i1:32,64 c1:32,64 g1:32,64 z1:32,64 zt1:32,64 "
-         "ln1:32,32 lt1:32,32 bs1:32,1 s1a:32,52 s1b:32,38 s1:32,12 sm1:128,25 cm2:32,384 sg2:32,1 bm2:32,32 row2:128,32 "
-         "cn2:128,25 cu2:128,25 sh2:128,25 de2:128,25 seg:128,125 sa2:128,50 sb2:128,25 sc2:128,25 a3:32,64 b3:32,64 c3:32,64 "
-         "na3:32,1 la3:32,30 lb3:32,30 lc3:32,32 lt3:32,32 bs3:32,1 g3:32,64 h3:32,64 k3:32,64 pk3:32,64 pl3:32,64 cx3:32,5,10 "
-         "cr3:32,5,10 cn3:32,25 in3:32,25 x3:32,25 xm3:32,25 xs3:32,10 xt3:32,5 xu3:32,5 sg3:32,320 sa3:32,128 sb3:32,64 sc3:32,64 "
-         "tq3:128,32 tr0:128,32 sm3:128,24 su3:32,96",
+    F32: "ys:128,768 cst:128,256 ct:128,128 ct2:128,128 fr:128,192 lm:32,32 tf:128,192 uf:128,192 ones:128,125 rst:128,125 tc0:128,5 "
+         "tcw:128,5 sa0:32,30 sam:32,30 lsa:32,30 ms0:32,25 ms3:32,25 ab0:32,96 ab1:32,96 i1:32,64 c1:32,64 g1:32,96 z1:32,64 "
+         "zt1:32,64 ln1:32,32 s1:32,60 sm1:128,25 cm2:32,384 sg2:32,1 bm2:128,32 row2:128,32 "
+         "cn2:128,25 cu2:128,25 sh2:128,25 de2:128,25 seg:128,125 ss2:128,125 aa3:32,128 bb3:32,128 c3:32,64 "
+         "na3:32,1 la3:32,64 g3:32,128 h3:32,64 k3:32,64 pk3:32,64 pl3:32,64 cx3:32,5,10 "
+         "cr3:32,5,10 cn3:32,25 in3:32,25 x3:32,25 xm3:32,25 xu3:32,25 sg3:32,320 sa3:32,128 sb3:32,64 sc3:32,64 "
+         "tq3:128,32 tr0:128,32 su3:32,120 sv3:32,120",
 }
 SCRATCH = {"ps": ("psum", [128, 2048], F32), "lists": ("dram", [N, 128, 3], I32)}
 for _t in SMALL:
     for _b in SMALL[_t].split():
         SCRATCH[_b.split(":")[0]] = ("sbuf", [int(_n) for _n in _b.split(":")[1].split(",")], _t)
-SEMAPHORES = ["v", "w", "ga", "gb", "gd", "d_e1", "d_x", "d_w", "d_l", "d_e2", "d_e3", "d_t3", "d_o1", "d_v3", "d_o2",
+SEMAPHORES = ["v", "w", "ga", "gb", "ge", "gd", "d_e1", "d_x", "d_w", "d_l", "d_e2", "d_e3", "d_t3", "d_o1", "d_v3", "d_o2",
               "sl", "s1c", "s1p", "s2c", "s2p", "loc", "ap", "m0", "m1", "m2", "m3", "ac", "st", "st2"]
 
 
@@ -41,7 +41,7 @@ def rank_program(g, core, T, topo):
     op = AluOpType
     X, COPY, LINE = AxisListType.X, ActivationFunctionType.Copy, ActivationFunctionType.Identity
     others = [r for r in range(N) if r != me]
-    cnt = {"v": 0, "w": 0, "ac": 0, "ga": 0, "gb": 0, "gd": 0}
+    cnt = {"v": 0, "w": 0, "ac": 0, "ga": 0, "gb": 0, "ge": 0, "gd": 0}
     CALL = {"ts": V.tensor_scalar, "tt": V.tensor_tensor, "cp": V.tensor_copy, "ms": V.memset, "red": V.tensor_reduce,
             "scan": V.tensor_tensor_scan, "tr": V.transpose, "qz": V.quantize_mx}
 
@@ -77,7 +77,7 @@ def rank_program(g, core, T, topo):
         cnt[line] += 1
 
     for d in range(N):
-        (g.sync if d % 2 else A).dma_start(T.e1[H * d:H * d + H, :], T.to[:]).then_inc(S.d_e1, 16)
+        (g.sync if d % 2 else A).dma_start(T.e1[d:N * H:N, :], T.to[:]).then_inc(S.d_e1, 16)
     g.sync.dma_start(T.lists[me], T.to[:]).then_inc(S.d_l, 16)
     g.sync.dma_start(T.xt[:, 0:768], T.x[:, 0:768]).then_inc(S.d_x, 16)
     A.dma_start(T.xt[:, 768:1536], T.x[:, 768:1536]).then_inc(S.d_x, 16)
@@ -85,27 +85,21 @@ def rank_program(g, core, T, topo):
 
     z0 = vf("ms", T.cst[:], 0.0)
     v("ms", T.z1[:], 0.0)
-    vf("ms", T.ln1[:], 0.0)
-    vf("ms", T.win1[:], 0.0)
+    for b in ("ln1", "ab1", "win1", "bm2", "bb3", "la3"):
+        vf("ms", T[b][:], 0.0)
+    nz = vf("ms", T.t3[:], 0)
     g.wait_ge(S.v, z0)
-    iota("ga", T.cst[0:32, 32:62], [[COLS, N], [0, H]])
-    iota("ga", T.cst[0:32, 64:94], [[COLS, N], [0, H]], COLS)
+    iota("ga", T.cst[0:32, 32:62], [[0, H], [COLS, N]])
+    iota("ga", T.cst[0:32, 64:94], [[0, H], [COLS, N]], COLS)
+    iota("ga", T.cst[0:32, 96:126], [[1, H], [H, N]])
     iota("ga", T.cst[:, 0:32], [[32, 2], [0, 16]])
-    iota("ga", T.cst[0:32, 96:126], [[COLS, N + 1], [0, N]])
-    iota("ga", T.cst[0:32, 128:158], [[0, N + 1], [5 * SLOT, N]])
-    iota("ga", T.cst[0:32, 160:190], [[SLOT, N], [0, H]], WHOLE - 200)
-    iota("ga", T.cst[:, 192:224], [[0, 2], [1, 16]])
-    iota("gb", T.ones[:], [[0, 64]], 1)
+    iota("gb", T.ones[:], [[0, 125]], 1)
     iota("gb", T.fr[:], [[64, 2], [2 * W, H], [2, 16]], -23)
-    sel("gb", False, T.lm[:], T.ones[0:32, 0:32], [[1, 32]], op.is_gt, 0, -1)
+    sel("gb", False, T.rst[:], T.ones[:], [[0, 25], [1, 5]], op.is_gt, 0, 0)
     V.wait_ge(S.ga, cnt["ga"])
-    nct = v("tr", T.ct[:], T.cst[:])
-    V.wait_ge(S.gb, cnt["gb"])
-    V.wait_ge(S.v, nct)
-    wf("ts", T.qf[:], T.fr[:], T.ct[:, 0:1], op.add, 1.0 / 48, op.mult)
-    wf("ts", T.tf[:], T.fr[:], T.ct[:, 0:1], op.add, 8.0, op.mult)
-    w("ts", T.uf[:], T.qf[:], -383.0, op.mult, -8.0, op.add)
-    w("tt", T.val1[:], T.tf[:], T.uf[:], op.add)
+    v("tr", T.ct[:], T.cst[:, 0:128])
+    R = slice(0, 30)
+    v("ts", T.lm[R, :], T.cst[R, 96:128], T.ct[R, 96:97], op.is_gt)
 
     per = len(topo.engines(core, T.cores[others[0]])) // len(others)
     landed = per * len(others)
@@ -121,11 +115,11 @@ def rank_program(g, core, T, topo):
     g.wait_ge(S.d_l, 16)
     spread(lambda r: T.lists[me], T.lists[me], S.sl)
 
-    iota("gd", T.t3[:], [[0, 32]])
-    iota("gd", T.bm2[:], [[0, 32]])
-    sel("gd", True, T.rst[:], T.ones[:, 0:25], [[0, 5], [1, 5]], op.is_gt, 0, 0)
-    iota("gd", T.tc0[:], [[16, 5]])
-    iota("gd", T.lc3[:], [[0, 32]])
+    iota("ge", T.cst[0:32, 128:158], [[COLS, N + 1], [0, N]])
+    iota("ge", T.cst[0:32, 160:190], [[0, N + 1], [5 * SLOT, N]])
+    iota("ge", T.cst[0:32, 192:222], [[SLOT, N], [0, H]], WHOLE - 200)
+    iota("ge", T.cst[:, 224:256], [[0, 2], [1, 16]])
+    iota("ge", T.tc0[:], [[16, 5]])
     sel("gd", True, T.sa0[:], T.ones[0:32, 0:30], [[-H, 5], [0, H]], op.is_ge, 0, 1)
     sel("gd", True, T.ms0[:], T.ones[0:32, 0:25], [[0, 5], [-H, 5]], op.is_ge, 0, 1)
     sel("gd", False, T.sam[:], T.sa0[:], [[H, 5], [0, H]], op.is_ge, H - 1, -1)
@@ -134,36 +128,39 @@ def rank_program(g, core, T, topo):
     iota("gd", T.val3[:], [[0, COLS]])
     iota("gd", T.win3[:, COLS * me:COLS * me + COLS], [[0, COLS]])
 
-    R = slice(0, 30)
     V.wait_ge(S.d_e1, 80)
-    vf("ts", T.a1[R, :], T.e1[R, :], T.ct[R, 32:33], op.is_ge)
-    vf("ts", T.b1[R, :], T.e1[R, :], T.ct[R, 64:65], op.is_ge)
-    v("scan", T.c1[R, :], T.a1[R, :], T.b1[R, :], 0.0, op.add, op.subtract)
+    v("ts", T.ab0[R, 32:96], T.e1[R, :], T.ct[R, 32:33], op.is_ge)
+    vf("ts", T.ab1[R, 32:96], T.e1[R, :], T.ct[R, 64:65], op.is_ge)
+    v("scan", T.c1[R, :], T.ab0[R, 32:96], T.ab1[R, 32:96], 0.0, op.add, op.subtract)
+    wf("tt", T.i1[R, :], T.ab0[R, 32:96], T.ab1[R, 32:96], op.subtract)
     v("ts", T.ln1[R, :], T.lm[R, :], T.c1[R, W - 1:W], op.mult)
-    wf("tt", T.i1[R, :], T.a1[R, :], T.b1[R, :], op.subtract)
-    v("tr", T.lt1[:], T.ln1[:])
-    v("red", T.bs1[:], T.lt1[:], X, op.add)
-    v("ts", T.g1[R, :], T.c1[R, :], T.bs1[R, 0:1], op.add)
-    V.wait_ge(S.w, cnt["w"])
-    v("tt", T.z1[R, :], T.g1[R, :], T.i1[R, :], op.mult)
+    V.wait_ge(S.gb, cnt["gb"])
+    wf("ts", T.qf[:], T.fr[:], T.ct[:, 0:1], op.add, 1.0 / 48, op.mult)
+    v("tr", T.ab0[:, 0:32], T.ln1[:])
+    wf("ts", T.tf[:], T.fr[:], T.ct[:, 0:1], op.add, 8.0, op.mult)
+    v("scan", T.g1[R, :], T.ab0[R, :], T.ab1[R, :], 0.0, op.add, op.subtract)
+    w("ts", T.uf[:], T.qf[:], -383.0, op.mult, -8.0, op.add)
+    v("tt", T.z1[R, :], T.g1[R, 32:96], T.i1[R, :], op.mult)
+    w("tt", T.val1[:], T.tf[:], T.uf[:], op.add)
     v("tr", T.zt1[:], T.z1[:])
 
     def pack(b):
         return wf("qz", T.q[:, 128 * b:128 * b + 128], T.p[:, 128 * b:128 * b + 128], T.xt[:, 512 * b:512 * b + 512])
-    v("tt", T.s1a[:], T.zt1[:, 0:52], T.zt1[:, 12:64], op.add)
     V.wait_ge(S.d_x, 32)
     pack(0)
-    v("tt", T.s1b[:], T.s1a[:, 0:38], T.s1a[:, 6:44], op.add)
+    v("scan", T.s1[:, 0:30], T.rst[0:32, 0:30], T.zt1[:, 0:30], 0.0, op.mult, op.add)
+    vf("scan", T.s1[:, 30:60], T.rst[0:32, 0:30], T.zt1[:, 32:62], 0.0, op.mult, op.add)
     pack(1)
-    v("tt", T.s1[:, 0:6], T.s1b[:, 0:6], T.zt1[:, 24:30], op.add)
-    vf("tt", T.s1[:, 6:12], T.s1b[:, 32:38], T.zt1[:, 56:62], op.add)
-    n1 = pack(2)
-    v("ts", T.of1[0:32, :], T.s1[:], -1.0, op.add)
+    v("ts", T.of1[0:32, :], T.s1[:, 4:60:5], -1.0, op.add)
     for a in range(1, 4):
-        vf("ts", T.of1[32 * a:32 * a + 32, :], T.s1[:], -1.0, op.add)
+        vf("ts", T.of1[32 * a:32 * a + 32, :], T.s1[:, 4:60:5], -1.0, op.add)
+    n1 = pack(2)
+    V.wait_ge(S.w, n1)
     nw1 = v("cp", T.win1[:, 0:400].indirect(T.of1[:, 0:12]), T.val1[:])
-    V.wait_ge(S.v, nw1)
     A.wait_ge(S.v, nw1)
+    V.wait_ge(S.ge, cnt["ge"])
+    wf("tr", T.ct2[:], T.cst[:, 128:256])
+    V.wait_ge(S.v, nw1)
     for k in range(N):
         for u in (0, 16):
             out, in_ = T.dup1[:, 5 * k:5 * k + 5, u:u + 16], T.win1[:, k:400:5]
@@ -173,9 +170,9 @@ def rank_program(g, core, T, topo):
                 nd1 = act(True, out, in_, COPY)
     V.wait_ge(S.ac, nd1)
     v("tr", T.tr1[:], T.dup1[:])
+    w("ts", T.tcw[:], T.tc0[:], T.ct2[:, 96:97], op.add)
     v("tt", T.sm1[:], T.tr1[:, 0:800:32], T.tr1[:, 16:800:32], op.add)
     nl1 = v("ts", T.l1[:, 0:25], T.sm1[:], 192.0, op.add)
-    V.wait_ge(S.w, n1)
     k1 = v("cp", T.q2[:].bitcast(dt.uint32), T.q[:].bitcast(dt.uint32).indirect(T.l1[:, 0:25]))
     A.wait_ge(S.w, n1)
     A.wait_ge(S.v, nl1)
@@ -187,12 +184,12 @@ def rank_program(g, core, T, topo):
     g.wait_ge(S.ap, 1)
     spread(lambda r: T.p2[:, cut(r, SENT1)], T.pl[:, cut(me, SENT1)], S.s1p)
 
+    g.sync.wait_ge(S.v, nz)
     g.sync.wait_ge(S.sl, landed)
     g.sync.wait_ge(S.d_l, 16)
     for d in range(N + 1):
         g.sync.dma_start(T.e2[N * d:N * d + N, :], T.lists[:]).then_inc(S.d_e2, 16)
     g.sync.dma_start(T.e3[R, :], T.lists[:]).then_inc(S.d_e3, 16)
-    g.sync.wait_ge(S.gd, cnt["gd"])
     for b in range(8):
         g.sync.dma_start(T.t3[32 * (b // 2):32 * (b // 2) + 24, 16 * (b % 2):16 * (b % 2) + 16], T.lists[b % N]).then_inc(S.d_t3, 16)
     g.sync.wait_ge(S.v, k1)
@@ -205,50 +202,42 @@ def rank_program(g, core, T, topo):
 
     def third():
         V.wait_ge(S.d_e3, 16)
-        w("ts", T.a3[R, :], T.e3[R, :], lo, op.is_ge)
-        wf("ts", T.b3[R, :], T.e3[R, :], lo + COLS, op.is_ge)
+        w("ts", T.aa3[R, 64:128], T.e3[R, :], lo, op.is_ge)
+        wf("ts", T.bb3[R, 64:128], T.e3[R, :], lo + COLS, op.is_ge)
         yield
-        w("scan", T.c3[R, :], T.a3[R, :], T.b3[R, :], 0.0, op.add, op.subtract)
-        wf("red", T.na3[R, :], T.a3[R, :], X, op.add)
+        w("scan", T.c3[R, :], T.aa3[R, 64:128], T.bb3[R, 64:128], 0.0, op.add, op.subtract)
+        wf("red", T.na3[R, :], T.aa3[R, 64:128], X, op.add)
         yield
-        w("ts", T.la3[R, :], T.lsa[R, :], T.c3[R, W - 1:W], op.mult)
-        wf("ts", T.lb3[R, :], T.sam[R, :], T.na3[R, 0:1], op.mult)
-        yield
-        w("tt", T.lc3[R, 0:30], T.la3[R, :], T.lb3[R, :], op.subtract)
+        w("ts", T.la3[R, 0:30], T.lsa[R, :], T.c3[R, W - 1:W], op.mult)
+        wf("ts", T.la3[R, 32:62], T.sam[R, :], T.na3[R, 0:1], op.mult, -1.0, op.mult)
         V.wait_ge(S.d_t3, 128)
         wf("cp", T.tq3[:], T.t3[:])
         yield
-        w("tr", T.lt3[:], T.lc3[:])
+        w("tr", T.aa3[:, 0:64], T.la3[:])
         wf("tr", T.tr0[:], T.tq3[:])
         yield
-        w("red", T.bs3[:], T.lt3[:], X, op.add)
+        w("scan", T.g3[R, :], T.aa3[R, :], T.bb3[R, :], 0.0, op.add, op.subtract)
         wf("cp", T.of3[:], T.tr0[:, 0:24])
         yield
-        w("ts", T.g3[R, :], T.c3[R, :], T.bs3[R, 0:1], op.add)
+        w("ts", T.pp3[R, :], T.g3[R, 64:128], 0.2, op.mult, 76.2, op.add)
         V.wait_ge(S.ac, mark["nc3"])
         wf("tt", T.cn3[:], T.cr3[:, :, 5:10], T.cr3[:, :, 0:5], op.subtract)
         yield
-        w("ts", T.pp3[R, :], T.g3[R, :], 0.2, op.mult, 76.2, op.add)
-        wf("scan", T.in3[:], T.rst[0:32, :], T.cn3[:], 0.0, op.mult, op.add)
-        yield
         w("ts", T.h3[R, :], T.pp3[R, :], -5.0, op.mult, 383.0, op.add)
+        wf("scan", T.in3[:], T.rst[0:32, 0:25], T.cn3[:], 0.0, op.mult, op.add)
+        yield
+        w("tt", T.k3[R, :], T.h3[R, :], T.g3[R, 64:128], op.add)
         wf("tt", T.x3[:], T.in3[:], T.cr3[:, :, 5:10], op.subtract)
         yield
-        w("tt", T.k3[R, :], T.h3[R, :], T.g3[R, :], op.add)
-        wf("tt", T.xm3[:], T.x3[:], T.ms3[:], op.mult)
+        w("tt", T.xm3[:], T.x3[:], T.ms3[:], op.mult)
+        wf("ts", T.pk3[R, :], T.k3[R, :], float(SLOT), op.mult, T.ct2[R, 64:65], op.add)
         yield
-        w("ts", T.pk3[R, :], T.k3[R, :], float(SLOT), op.mult, T.ct[R, 160:161], op.add)
-        wf("tt", T.xs3[:, 0:5], T.xm3[:, 0:25:5], T.xm3[:, 1:25:5], op.add)
-        wf("tt", T.xs3[:, 5:10], T.xm3[:, 2:25:5], T.xm3[:, 3:25:5], op.add)
-        yield
-        w("tt", T.xt3[:], T.xs3[:, 0:5], T.xs3[:, 5:10], op.add)
+        w("scan", T.xu3[:], T.rst[0:32, 0:25], T.xm3[:], 0.0, op.mult, op.add)
         wf("tt", T.pl3[R, :], T.pk3[R, :], T.pp3[R, :], op.add)
         yield
-        w("tt", T.xu3[:], T.xt3[:], T.xm3[:, 4:25:5], op.add)
-        yield
-        w("ts", T.sg3[R, 0:W], T.k3[R, :], 0.0, op.is_equal, T.xu3[R, 0:1], op.mult)
+        w("ts", T.sg3[R, 0:W], T.k3[R, :], 0.0, op.is_equal, T.xu3[R, 4:5], op.mult)
         for k in range(1, N):
-            wf("ts", T.sg3[R, W * k:W * k + W], T.k3[R, :], float(k), op.is_equal, T.xu3[R, k:k + 1], op.mult)
+            wf("ts", T.sg3[R, W * k:W * k + W], T.k3[R, :], float(k), op.is_equal, T.xu3[R, 5 * k + 4:5 * k + 5], op.mult)
         yield
         w("tt", T.sa3[R, :], T.sg3[R, 0:2 * W], T.sg3[R, 2 * W:4 * W], op.add)
         wf("tt", T.sc3[R, :], T.sg3[R, 4 * W:5 * W], T.pl3[R, :], op.add)
@@ -263,50 +252,46 @@ def rank_program(g, core, T, topo):
             if next(steps, 1) is not None:
                 return
 
-    V.wait_ge(S.gd, cnt["gd"])
-    wf("ts", T.tcw[:], T.tc0[:], T.ct[:, 192:193], op.add)
     V.wait_ge(S.d_e2, 96)
-    v("ts", T.cm2[R, :], T.e2[R, :], T.ct[R, 96:97], op.is_ge)
+    V.wait_ge(S.gd, cnt["gd"])
+    V.wait_ge(S.w, cnt["w"])
+    v("ts", T.cm2[R, :], T.e2[R, :], T.ct2[R, 0:1], op.is_ge)
     step()
     v("red", T.sg2[R, :], T.cm2[R, :], X, op.add)
     step()
-    v("ts", T.bm2[R, :], T.ones[R, 0:32], T.sg2[R, 0:1], op.mult, T.ct[R, 128:129], op.subtract)
+    v("ts", T.bm2[R, :], T.ones[R, 0:32], T.sg2[R, 0:1], op.mult, T.ct2[R, 32:33], op.subtract)
+    for a in range(1, 4):
+        vf("ts", T.bm2[32 * a:32 * a + 30, :], T.ones[R, 0:32], T.sg2[R, 0:1], op.mult, T.ct2[R, 32:33], op.subtract)
     step()
-    nrow = v("tr", T.row2[0:32, :], T.bm2[:])
+    nrow = v("tr", T.row2[:], T.bm2[:])
     A.wait_ge(S.v, nrow)
     for k in range(N):
         act(True, T.cx3[:, k, :], T.row2[0:32, 5 * me:5 * me + 10], LINE, scale=-0.2, bias=(386 - k) * 0.2)
     mark["nc3"] = act(False, T.cr3[:], T.cx3[:], LINE, bias=float(WHOLE))
     step()
-    v("cp", T.row2[32:64, :], T.row2[0:32, :])
-    vf("cp", T.row2[64:96, :], T.row2[0:32, :])
-    vf("cp", T.row2[96:128, :], T.row2[0:32, :])
     v("ts", T.ci2[:], T.row2[:, 0:30], -0.2, op.mult, (386 - me) * 0.2, op.add)
     step()
     v("tt", T.cn2[:], T.ci2[:, 5:30], T.ci2[:, 0:25], op.subtract)
-    vf("tt", T.sh2[:], T.ci2[:, 4:29], T.rst[:], op.mult)
+    vf("tt", T.sh2[:], T.ci2[:, 4:29], T.rst[:, 0:25], op.mult)
     step()
-    v("scan", T.cu2[:], T.rst[:], T.cn2[:], 0.0, op.mult, op.add)
+    v("scan", T.cu2[:], T.rst[:, 0:25], T.cn2[:], 0.0, op.mult, op.add)
     nde = vf("tt", T.de2[:], T.ci2[:, 0:25], T.sh2[:], op.subtract)
     step()
     V.wait_ge(S.v, nde)
     A.wait_ge(S.v, nde)
     for r in range(N):
         for d in range(N):
-            out, e = T.seg[:, 25 * r + 5 * d:25 * r + 5 * d + 5], T.de2[:, 5 * d + r:5 * d + r + 1]
+            out, e = T.seg[:, 25 * d + r:25 * d + 25:5], T.de2[:, 5 * d + r:5 * d + r + 1]
             if r == 0:
                 nsg = act(d > 0, out, T.tcw[:], LINE, bias=e)
             else:
                 vf("ts", out, T.tcw[:], T.cu2[:, 5 * d + r - 1:5 * d + r], op.is_ge, e, op.mult)
     step()
     V.wait_ge(S.ac, nsg)
-    v("tt", T.sa2[:], T.seg[:, 0:50], T.seg[:, 50:100], op.add)
+    v("scan", T.ss2[:], T.rst[:], T.seg[:], 0.0, op.mult, op.add)
     step()
-    v("tt", T.sb2[:], T.sa2[:, 0:25], T.sa2[:, 25:50], op.add)
+    n2 = v("ts", T.l2[:, 0:25], T.ss2[:, 4:125:5], float(SLOT * (N - 1) + SENT1 - 1), op.min)
     step()
-    v("tt", T.sc2[:], T.sb2[:], T.seg[:, 100:125], op.add)
-    step()
-    n2 = v("ts", T.l2[:, 0:25], T.sc2[:], float(SLOT * (N - 1) + SENT1 - 1), op.min)
 
     V.wait_ge(S.s1c, landed)
     V.wait_ge(S.d_o1, 32)
@@ -335,14 +320,13 @@ def rank_program(g, core, T, topo):
     w("cp", T.dup3[:, :, 0:16], mine)
     wf("cp", T.dup3[:, :, 16:32], mine)
     w("tr", T.tr3[:], T.dup3[:])
-    w("tt", T.sm3[:], T.tr3[:, 0:768:32], T.tr3[:, 16:768:32], op.add)
-    w("cp", T.su3[:, 0:24], T.sm3[32:64, :])
-    wf("cp", T.su3[:, 24:48], T.sm3[64:96, :])
-    w("tt", T.su3[:, 48:72], T.sm3[0:32, :], T.su3[:, 0:24], op.add)
-    w("tt", T.su3[:, 72:96], T.su3[:, 48:72], T.su3[:, 24:48], op.add)
-    w("ts", T.l3[0:32, :], T.su3[:, 72:96], 200.0, op.add)
+    V.wait_ge(S.w, cnt["w"])
+    for r in range(N):
+        wf("cp", T.su3[:, r:120:5], T.tr3[32 * (r // 2):32 * (r // 2) + 32, 16 * (r % 2):768:32])
+    w("scan", T.sv3[:], T.rst[0:32, 0:120], T.su3[:], 0.0, op.mult, op.add)
+    w("ts", T.l3[0:32, :], T.sv3[:, 4:120:5], 200.0, op.add)
     for a in range(1, 4):
-        n3 = wf("ts", T.l3[32 * a:32 * a + 32, :], T.su3[:, 72:96], 200.0, op.add)
+        n3 = wf("ts", T.l3[32 * a:32 * a + 32, :], T.sv3[:, 4:120:5], 200.0, op.add)
 
     V.wait_ge(S.s2c, landed)
     V.wait_ge(S.d_o2, 32)
@@ -354,7 +338,7 @@ def rank_program(g, core, T, topo):
     for h in range(2):
         c = slice(HALF * h, HALF * h + HALF)
         off = T.l3[:, 12 * h:12 * h + 12]
-        nk = v("cp", T.q4[:, c].bitcast(dt.uint32), T.qm[:].bitcast(dt.uint32).indirect(off))
+        nk = vec("v", h > 0, "cp", (T.q4[:, c].bitcast(dt.uint32), T.qm[:].bitcast(dt.uint32).indirect(off)))
         A.activation(T.p4[:, c], T.pm[:].indirect(off), COPY).then_inc(S.ap, 1)
         g.tensor.wait_ge(S.v, nk)
         g.tensor.wait_ge(S.ap, 3 + h)

@@ -1,36 +1,35 @@
 from concourse.bass import DstId, RemoteDMATransfer
-from concourse.mybir import dt, AluOpType, AxisListType, ActivationFunctionType
+from concourse.mybir import dt, AluOpType, ActivationFunctionType
 
 N, COLS = 5, 384
 SLOT = 80
-SENT1 = 77
+SENT1 = 78
 H = 6
 W = COLS // H
-WHOLE = 3 << 22
+STEP = 1024.0
 
 F32, BF, I32, U16 = "float32", "bfloat16", "int32", "uint16"
 X4, U8 = "float8_e4m3fn_x4", "uint8"
 SMALL = {
     X4: "q:128,384 wq:128,256 q2:128,400 ql:128,400 q3:128,400 qm:128,400 q4:128,384",
     U8: "p:128,384 wp:128,256 p2:128,400 pl:128,400 p3:128,400 pm:128,400 p4:128,384",
-    BF: "xt:128,1536 wt:128,1024 val1:128,192 win1:128,400 dup1:128,25,32 tr1:128,800 v3:32,64 val3:128,384 win3:128,1920 "
-        "dup3:128,24,32 tr3:128,768",
-    I32: "qf:128,192 e1:32,64 e2:32,384 ci2:128,30 e3:32,64 pp3:32,64 t3:128,32",
-    U16: "of1:128,12 l1:128,26 l2:128,26 of3:128,24 l3:128,24",
-    F32: "ys:128,768 cst:128,256 ct:128,128 ct2:128,128 fr:128,192 lm:32,32 tf:128,192 uf:128,192 ones:128,125 rst:128,125 tc0:128,5 "
-         "tcw:128,5 sa0:32,30 sam:32,30 lsa:32,30 ms0:32,25 ms3:32,25 ab0:32,96 ab1:32,96 i1:32,64 c1:32,64 g1:32,96 z1:32,64 "
-         "zt1:32,64 ln1:32,32 s1:32,60 sm1:128,25 cm2:32,384 sg2:32,1 bm2:128,32 row2:128,32 "
-         "cn2:128,25 cu2:128,25 sh2:128,25 de2:128,25 seg:128,125 ss2:128,125 aa3:32,128 bb3:32,128 c3:32,64 "
-         "na3:32,1 la3:32,64 g3:32,128 h3:32,64 k3:32,64 pk3:32,64 pl3:32,64 cx3:32,5,10 "
-         "cr3:32,5,10 cn3:32,25 in3:32,25 x3:32,25 xm3:32,25 xu3:32,25 sg3:32,320 sa3:32,128 sb3:32,64 sc3:32,64 "
-         "tq3:128,32 tr0:128,32 su3:32,120 sv3:32,120",
+    BF: "xt:128,1536 wt:128,1024 nat:128,6,64 val1:128,192 win1:128,400 dup1:128,25,32 tr1:128,800 v3:32,64 val3:128,320 "
+        "win3:128,1920 dup3:128,24,32 tr3:128,768 cs2:128,50",
+    I32: "l0:16,24 e1:32,64 ci2:128,25 pp3:32,64 qq3:32,64",
+    U16: "of1:128,12 l1:128,26 l2:128,26 of3:128,20 l3:128,24",
+    F32: "ys:128,768 lf:16,24 lo_r:32,35 key_r:32,35 thr_r:32,35 run_r:32,35 q_r:128,32 lo_c:32,32 key_c:32,32 thr_c:32,32 "
+         "run_c:32,32 q_c:128,32 ones:128,144 rst:128,125 rst6:32,144 rst2:128,50 tc0:128,5 tcw:128,5 tcb:128,5 lm:32,32 sa0:32,30 "
+         "sam:32,30 lsa:32,30 lst:32,30 mr0:32,5 mr:32,5 mx:32,5 ab0:32,96 ab1:32,96 c1:32,64 ln1:32,32 g1:32,96 z1:32,64 zt1:32,64 "
+         "s1:32,60 sm1:128,25 e2:32,384 jk2:32,384 sg2:32,1 bm2:128,32 row2:128,32 nn2:128,25 o2:128,50 off2:128,25 gx2:128,125 "
+         "fx2:128,125 ss2:128,125 e3:32,64 u3:32,64 na3:32,1 la3:32,32 aa3:32,96 bb3:32,96 g3:32,96 gv3:32,64 xo3:32,10 jk3:32,16 "
+         "cp3:32,1 cv3:32,1 tp3:32,64 ts3:32,64 t3:128,32 tr0:128,32 su3:32,144 sv3:32,144",
 }
-SCRATCH = {"ps": ("psum", [128, 2048], F32), "lists": ("dram", [N, 128, 3], I32)}
+SCRATCH = {"ps": ("psum", [128, 2048], F32), "lists": ("dram", [N, 128, 3], F32)}
 for _t in SMALL:
     for _b in SMALL[_t].split():
         SCRATCH[_b.split(":")[0]] = ("sbuf", [int(_n) for _n in _b.split(":")[1].split(",")], _t)
-SEMAPHORES = ["v", "w", "ga", "gb", "ge", "gd", "d_e1", "d_x", "d_w", "d_l", "d_e2", "d_e3", "d_t3", "d_o1", "d_v3", "d_o2",
-              "sl", "s1c", "s1p", "s2c", "s2p", "loc", "ap", "m0", "m1", "m2", "m3", "ac", "st", "st2"]
+SEMAPHORES = ["v", "w", "ac", "ap", "ga", "gb", "gn", "ge", "gd", "d_e1", "d_x", "d_w", "d_l", "d_lf", "d_e2", "d_e3", "d_t3",
+              "d_o1", "d_v1", "d_v3", "d_o2", "sl", "s1c", "s1p", "s2c", "s2p", "loc", "m0", "m1", "m2", "m3", "st", "st2"]
 
 
 def rank_program(g, core, T, topo):
@@ -38,11 +37,11 @@ def rank_program(g, core, T, topo):
     if me is None:
         return
     S, V, A = T.sem, g.vector, g.scalar
-    op = AluOpType
-    X, COPY, LINE = AxisListType.X, ActivationFunctionType.Copy, ActivationFunctionType.Identity
+    op, FN = AluOpType, ActivationFunctionType
+    COPY, LINE = FN.Copy, FN.Identity
     others = [r for r in range(N) if r != me]
-    cnt = {"v": 0, "w": 0, "ac": 0, "ga": 0, "gb": 0, "ge": 0, "gd": 0}
-    CALL = {"ts": V.tensor_scalar, "tt": V.tensor_tensor, "cp": V.tensor_copy, "ms": V.memset, "red": V.tensor_reduce,
+    cnt = {"v": 0, "w": 0, "ac": 0, "ga": 0, "gb": 0, "gn": 0, "ge": 0, "gd": 0}
+    CALL = {"ts": V.tensor_scalar, "tt": V.tensor_tensor, "cp": V.tensor_copy, "ms": V.memset,
             "scan": V.tensor_tensor_scan, "tr": V.transpose, "qz": V.quantize_mx}
 
     def vec(line, free, name, args):
@@ -59,9 +58,7 @@ def rank_program(g, core, T, topo):
     w = lambda name, *args: vec("w", False, name, args)
     wf = lambda name, *args: vec("w", True, name, args)
 
-    def act(free, out, in_, func, **k):
-        if cnt["ac"] and not free:
-            A.wait_ge(S.ac, cnt["ac"])
+    def act(out, in_, func, **k):
         A.activation(out, in_, func, **k).then_inc(S.ac, 1)
         cnt["ac"] += 1
         return cnt["ac"]
@@ -70,36 +67,47 @@ def rank_program(g, core, T, topo):
         g.iota(out, pattern, base, cm, allow_small_or_imprecise_dtypes=True).then_inc(S[line], 1)
         cnt[line] += 1
 
-    def sel(line, free, out, in_, pattern, how, base, cm):
-        if not free:
-            g.wait_ge(S[line], cnt[line])
+    def sel(line, out, in_, pattern, how, base, cm):
         g.affine_select(out, in_, pattern, how, 0.0, base, cm).then_inc(S[line], 1)
         cnt[line] += 1
+    R = slice(0, 30)
 
+    g.sync.dma_start(T.l0[:], T.to[:]).then_inc(S.d_l, 16)
     for d in range(N):
         (g.sync if d % 2 else A).dma_start(T.e1[d:N * H:N, :], T.to[:]).then_inc(S.d_e1, 16)
-    g.sync.dma_start(T.lists[me], T.to[:]).then_inc(S.d_l, 16)
     g.sync.dma_start(T.xt[:, 0:768], T.x[:, 0:768]).then_inc(S.d_x, 16)
     A.dma_start(T.xt[:, 768:1536], T.x[:, 768:1536]).then_inc(S.d_x, 16)
-    g.sync.dma_start(T.wt[:], T.w[:]).then_inc(S.d_w, 16)
+    A.dma_start(T.wt[:], T.w[:]).then_inc(S.d_w, 16)
 
-    z0 = vf("ms", T.cst[:], 0.0)
-    v("ms", T.z1[:], 0.0)
-    for b in ("ln1", "ab1", "win1", "bm2", "bb3", "la3"):
+    iota("ga", T.lo_r[:], [[0, H + 1], [COLS, N]])
+    iota("ga", T.key_r[:], [[1, H + 1], [H, N]])
+    nones = vf("ms", T.ones[:], 1.0)
+    for b in ("z1", "ln1"):
         vf("ms", T[b][:], 0.0)
-    nz = vf("ms", T.t3[:], 0)
-    g.wait_ge(S.v, z0)
-    iota("ga", T.cst[0:32, 32:62], [[0, H], [COLS, N]])
-    iota("ga", T.cst[0:32, 64:94], [[0, H], [COLS, N]], COLS)
-    iota("ga", T.cst[0:32, 96:126], [[1, H], [H, N]])
-    iota("ga", T.cst[:, 0:32], [[32, 2], [0, 16]])
-    iota("gb", T.ones[:], [[0, 125]], 1)
-    iota("gb", T.fr[:], [[64, 2], [2 * W, H], [2, 16]], -23)
-    sel("gb", False, T.rst[:], T.ones[:], [[0, 25], [1, 5]], op.is_gt, 0, 0)
+    vf("ms", T.ab1[:, 0:32], 0.0)
+    vf("ms", T.val1[:], 0.0)
     V.wait_ge(S.ga, cnt["ga"])
-    v("tr", T.ct[:], T.cst[:, 0:128])
-    R = slice(0, 30)
-    v("ts", T.lm[R, :], T.cst[R, 96:128], T.ct[R, 96:97], op.is_gt)
+    vf("tr", T.lo_c[:], T.lo_r[:, 0:32])
+    vf("tr", T.key_c[:], T.key_r[:, 0:32])
+    v("ts", T.lm[R, :], T.key_r[R, 0:32], T.key_c[R, 0:1], op.is_gt)
+    wf("ms", T.val3[:], 0.0)
+    iota("gn", T.nat[:], [[1, 16], [16, 24]], -192)
+    g.wait_ge(S.v, nones)
+    sel("gb", T.rst[:], T.ones[:, 0:125], [[0, 25], [1, 5]], op.is_gt, 0, 0)
+
+    V.wait_ge(S.d_e1, 80)
+    v("ts", T.ab0[R, 32:96], T.e1[R, :], T.lo_c[R, 0:1], op.is_ge)
+    nab = vf("ts", T.ab1[R, 32:96], T.e1[R, :], -float(COLS), op.add, T.lo_c[R, 0:1], op.is_ge)
+    V.wait_ge(S.d_l, 16)
+    nlf = wf("cp", T.lf[:], T.l0[:])
+    g.sync.wait_ge(S.w, nlf)
+    g.sync.dma_start(T.lists[me], T.lf[:]).then_inc(S.d_lf, 16)
+    g.sync.wait_ge(S.v, nab)
+    g.sync.wait_ge(S.gn, cnt["gn"])
+    for blk in range(2):
+        for odd in range(2):
+            g.sync.dma_start(T.val1[16 * odd:128:32, 96 * blk:96 * blk + 96],
+                             T.nat[16 * odd:128:32, :, 32 * blk + 16 * odd:32 * blk + 16 * odd + 16]).then_inc(S.d_v1, 16)
 
     per = len(topo.engines(core, T.cores[others[0]])) // len(others)
     landed = per * len(others)
@@ -112,54 +120,56 @@ def rank_program(g, core, T, topo):
             moves.append(RemoteDMATransfer(dst_ids=[DstId(rid=rid, pnc=pid)], dma_engine_mask=sum(1 << b for b in e),
                                            remote_sem=sem, srcs=[src(r)], dsts=[dst]))
         g.remote_dma_fused(moves, local_sem=S.loc)
-    g.wait_ge(S.d_l, 16)
+
+    iota("ge", T.thr_r[:], [[-2 * COLS, H + 1], [0, N]], 1)
+    iota("ge", T.run_r[:], [[0, H + 1], [-10 * SLOT, N]])
+    iota("ge", T.q_r[:], [[0, 2], [1, 16]])
+    iota("ge", T.tc0[:], [[16, 5]])
+    g.wait_ge(S.d_lf, 16)
     spread(lambda r: T.lists[me], T.lists[me], S.sl)
 
-    iota("ge", T.cst[0:32, 128:158], [[COLS, N + 1], [0, N]])
-    iota("ge", T.cst[0:32, 160:190], [[0, N + 1], [5 * SLOT, N]])
-    iota("ge", T.cst[0:32, 192:222], [[SLOT, N], [0, H]], WHOLE - 200)
-    iota("ge", T.cst[:, 224:256], [[0, 2], [1, 16]])
-    iota("ge", T.tc0[:], [[16, 5]])
-    sel("gd", True, T.sa0[:], T.ones[0:32, 0:30], [[-H, 5], [0, H]], op.is_ge, 0, 1)
-    sel("gd", True, T.ms0[:], T.ones[0:32, 0:25], [[0, 5], [-H, 5]], op.is_ge, 0, 1)
-    sel("gd", False, T.sam[:], T.sa0[:], [[H, 5], [0, H]], op.is_ge, H - 1, -1)
-    sel("gd", True, T.ms3[:], T.ms0[:], [[0, 5], [H, 5]], op.is_ge, H - 1, -1)
-    sel("gd", False, T.lsa[:], T.sam[:], [[1, 30]], op.is_gt, 0, -1)
-    iota("gd", T.val3[:], [[0, COLS]])
-    iota("gd", T.win3[:, COLS * me:COLS * me + COLS], [[0, COLS]])
+    sel("gd", T.sa0[:], T.ones[0:32, 0:30], [[-H, 5], [0, H]], op.is_ge, 0, 1)
+    sel("gd", T.mr0[:], T.ones[0:32, 0:5], [[-H, 5]], op.is_ge, 0, 1)
+    sel("gd", T.rst2[:], T.ones[:, 0:50], [[0, 5], [1, 10]], op.not_equal, -1, 0)
+    g.wait_ge(S.gd, cnt["gd"])
+    sel("gd", T.sam[:], T.sa0[:], [[H, 5], [0, H]], op.is_ge, H - 1, -1)
+    sel("gd", T.mr[:], T.mr0[:], [[H, 5]], op.is_ge, H - 1, -1)
+    g.wait_ge(S.gd, cnt["gd"])
+    sel("gd", T.lsa[:], T.sam[:], [[1, 30]], op.is_gt, 0, -1)
+    sel("gd", T.lst[:], T.sam[:], [[-1, 30]], op.is_gt, 0, 1)
+    sel("gd", T.rst6[:], T.ones[0:32, :], [[0, 24], [1, H]], op.is_gt, 0, 0)
 
-    V.wait_ge(S.d_e1, 80)
-    v("ts", T.ab0[R, 32:96], T.e1[R, :], T.ct[R, 32:33], op.is_ge)
-    vf("ts", T.ab1[R, 32:96], T.e1[R, :], T.ct[R, 64:65], op.is_ge)
     v("scan", T.c1[R, :], T.ab0[R, 32:96], T.ab1[R, 32:96], 0.0, op.add, op.subtract)
-    wf("tt", T.i1[R, :], T.ab0[R, 32:96], T.ab1[R, 32:96], op.subtract)
+    wf("ms", T.win1[:, 0:200], 0.0)
     v("ts", T.ln1[R, :], T.lm[R, :], T.c1[R, W - 1:W], op.mult)
-    V.wait_ge(S.gb, cnt["gb"])
-    wf("ts", T.qf[:], T.fr[:], T.ct[:, 0:1], op.add, 1.0 / 48, op.mult)
+    wf("ms", T.win1[:, 200:400], 0.0)
     v("tr", T.ab0[:, 0:32], T.ln1[:])
-    wf("ts", T.tf[:], T.fr[:], T.ct[:, 0:1], op.add, 8.0, op.mult)
+    for b in ("t3", "bm2", "la3"):
+        wf("ms", T[b][:], 0.0)
+    nz = cnt["w"]
     v("scan", T.g1[R, :], T.ab0[R, :], T.ab1[R, :], 0.0, op.add, op.subtract)
-    w("ts", T.uf[:], T.qf[:], -383.0, op.mult, -8.0, op.add)
-    v("tt", T.z1[R, :], T.g1[R, 32:96], T.i1[R, :], op.mult)
-    w("tt", T.val1[:], T.tf[:], T.uf[:], op.add)
-    v("tr", T.zt1[:], T.z1[:])
 
     def pack(b):
         return wf("qz", T.q[:, 128 * b:128 * b + 128], T.p[:, 128 * b:128 * b + 128], T.xt[:, 512 * b:512 * b + 512])
     V.wait_ge(S.d_x, 32)
     pack(0)
-    v("scan", T.s1[:, 0:30], T.rst[0:32, 0:30], T.zt1[:, 0:30], 0.0, op.mult, op.add)
-    vf("scan", T.s1[:, 30:60], T.rst[0:32, 0:30], T.zt1[:, 32:62], 0.0, op.mult, op.add)
+    v("tt", T.z1[R, :], T.g1[R, 32:96], T.ab0[R, 32:96], op.mult)
     pack(1)
+    v("tr", T.zt1[:], T.z1[:])
+    n1 = pack(2)
+    V.wait_ge(S.gb, cnt["gb"])
+    v("scan", T.s1[:, 0:30], T.rst[0:32, 0:30], T.zt1[:, 0:30], 0.0, op.mult, op.max)
+    vf("scan", T.s1[:, 30:60], T.rst[0:32, 0:30], T.zt1[:, 32:62], 0.0, op.mult, op.max)
+    wf("ms", T.cs2[:], -128.0)
     v("ts", T.of1[0:32, :], T.s1[:, 4:60:5], -1.0, op.add)
     for a in range(1, 4):
         vf("ts", T.of1[32 * a:32 * a + 32, :], T.s1[:, 4:60:5], -1.0, op.add)
-    n1 = pack(2)
     V.wait_ge(S.w, n1)
+    V.wait_ge(S.d_v1, 64)
     nw1 = v("cp", T.win1[:, 0:400].indirect(T.of1[:, 0:12]), T.val1[:])
     A.wait_ge(S.v, nw1)
     V.wait_ge(S.ge, cnt["ge"])
-    wf("tr", T.ct2[:], T.cst[:, 128:256])
+    nct = wf("tr", T.thr_c[:], T.thr_r[:, 0:32])
     V.wait_ge(S.v, nw1)
     for k in range(N):
         for u in (0, 16):
@@ -167,12 +177,15 @@ def rank_program(g, core, T, topo):
             if k < 3:
                 vf("cp", out, in_)
             else:
-                nd1 = act(True, out, in_, COPY)
+                nd1 = act(out, in_, COPY)
     V.wait_ge(S.ac, nd1)
     v("tr", T.tr1[:], T.dup1[:])
-    w("ts", T.tcw[:], T.tc0[:], T.ct2[:, 96:97], op.add)
+    wf("tr", T.q_c[:], T.q_r[:])
+    nrc = wf("tr", T.run_c[:], T.run_r[:, 0:32])
     v("tt", T.sm1[:], T.tr1[:, 0:800:32], T.tr1[:, 16:800:32], op.add)
+    w("ts", T.tcw[:], T.tc0[:], T.q_c[:, 0:1], op.add)
     nl1 = v("ts", T.l1[:, 0:25], T.sm1[:], 192.0, op.add)
+    w("ts", T.tcb[:], T.tcw[:], 0.5, op.add, STEP, op.mult)
     k1 = v("cp", T.q2[:].bitcast(dt.uint32), T.q[:].bitcast(dt.uint32).indirect(T.l1[:, 0:25]))
     A.wait_ge(S.w, n1)
     A.wait_ge(S.v, nl1)
@@ -184,115 +197,83 @@ def rank_program(g, core, T, topo):
     g.wait_ge(S.ap, 1)
     spread(lambda r: T.p2[:, cut(r, SENT1)], T.pl[:, cut(me, SENT1)], S.s1p)
 
-    g.sync.wait_ge(S.v, nz)
+    g.sync.wait_ge(S.w, nz)
     g.sync.wait_ge(S.sl, landed)
-    g.sync.wait_ge(S.d_l, 16)
+    g.sync.wait_ge(S.d_lf, 16)
     for d in range(N + 1):
         g.sync.dma_start(T.e2[N * d:N * d + N, :], T.lists[:]).then_inc(S.d_e2, 16)
     g.sync.dma_start(T.e3[R, :], T.lists[:]).then_inc(S.d_e3, 16)
+    g.sync.wait_ge(S.d_e3, 16)
     for b in range(8):
-        g.sync.dma_start(T.t3[32 * (b // 2):32 * (b // 2) + 24, 16 * (b % 2):16 * (b % 2) + 16], T.lists[b % N]).then_inc(S.d_t3, 16)
+        g.sync.dma_start(T.t3[32 * (b // 2):32 * (b // 2) + 20, 16 * (b % 2):16 * (b % 2) + 16],
+                         T.e3[5 * (b % H):5 * (b % H) + 5, :]).then_inc(S.d_t3, 16)
     g.sync.wait_ge(S.v, k1)
     g.sync.dma_start(T.ql[:, cut(me, SLOT)].bitcast(dt.uint8), T.q2[:, cut(me, SLOT)].bitcast(dt.uint8)).then_inc(S.d_o1, 16)
     g.sync.wait_ge(S.ap, 1)
     g.sync.dma_start(T.pl[:, cut(me, SLOT)], T.p2[:, cut(me, SLOT)]).then_inc(S.d_o1, 16)
 
-    lo = float(COLS * me)
-    mark = {}
+    A.wait_ge(S.d_e2, 96)
+    A.wait_ge(S.w, nct)
+    nsg = act(T.jk2[R, :], T.e2[R, :], FN.Sign, scale=2.0, bias=T.thr_c[R, 0:1], accum_out=T.sg2[R, 0:1])
+    A.wait_ge(S.d_e3, 16)
+    nu3 = act(T.u3[R, :], T.e3[R, :], FN.Abs, scale=2.0, bias=-float(2 * COLS * me + COLS - 1))
+    A.wait_ge(S.ac, nsg)
+    A.wait_ge(S.w, nrc)
+    for a in range(2):
+        nbm = act(T.bm2[32 * a:32 * a + 30, :], T.ones[R, 0:32], LINE, scale=T.sg2[R, 0:1], bias=T.run_c[R, 0:1])
+    A.wait_ge(S.ac, nu3)
+    ni3 = act(T.aa3[R, 32:96], T.u3[R, :], FN.Sign, scale=-1.0, bias=float(COLS), accum_out=T.na3[R, 0:1])
+    A.wait_ge(S.gd, cnt["gd"])
+    A.wait_ge(S.ac, ni3)
+    nla = act(T.la3[R, 0:30], T.lsa[R, :], LINE, scale=T.na3[R, 0:1])
 
-    def third():
-        V.wait_ge(S.d_e3, 16)
-        w("ts", T.aa3[R, 64:128], T.e3[R, :], lo, op.is_ge)
-        wf("ts", T.bb3[R, 64:128], T.e3[R, :], lo + COLS, op.is_ge)
-        yield
-        w("scan", T.c3[R, :], T.aa3[R, 64:128], T.bb3[R, 64:128], 0.0, op.add, op.subtract)
-        wf("red", T.na3[R, :], T.aa3[R, 64:128], X, op.add)
-        yield
-        w("ts", T.la3[R, 0:30], T.lsa[R, :], T.c3[R, W - 1:W], op.mult)
-        wf("ts", T.la3[R, 32:62], T.sam[R, :], T.na3[R, 0:1], op.mult, -1.0, op.mult)
-        V.wait_ge(S.d_t3, 128)
-        wf("cp", T.tq3[:], T.t3[:])
-        yield
-        w("tr", T.aa3[:, 0:64], T.la3[:])
-        wf("tr", T.tr0[:], T.tq3[:])
-        yield
-        w("scan", T.g3[R, :], T.aa3[R, :], T.bb3[R, :], 0.0, op.add, op.subtract)
-        wf("cp", T.of3[:], T.tr0[:, 0:24])
-        yield
-        w("ts", T.pp3[R, :], T.g3[R, 64:128], 0.2, op.mult, 76.2, op.add)
-        V.wait_ge(S.ac, mark["nc3"])
-        wf("tt", T.cn3[:], T.cr3[:, :, 5:10], T.cr3[:, :, 0:5], op.subtract)
-        yield
-        w("ts", T.h3[R, :], T.pp3[R, :], -5.0, op.mult, 383.0, op.add)
-        wf("scan", T.in3[:], T.rst[0:32, 0:25], T.cn3[:], 0.0, op.mult, op.add)
-        yield
-        w("tt", T.k3[R, :], T.h3[R, :], T.g3[R, 64:128], op.add)
-        wf("tt", T.x3[:], T.in3[:], T.cr3[:, :, 5:10], op.subtract)
-        yield
-        w("tt", T.xm3[:], T.x3[:], T.ms3[:], op.mult)
-        wf("ts", T.pk3[R, :], T.k3[R, :], float(SLOT), op.mult, T.ct2[R, 64:65], op.add)
-        yield
-        w("scan", T.xu3[:], T.rst[0:32, 0:25], T.xm3[:], 0.0, op.mult, op.add)
-        wf("tt", T.pl3[R, :], T.pk3[R, :], T.pp3[R, :], op.add)
-        yield
-        w("ts", T.sg3[R, 0:W], T.k3[R, :], 0.0, op.is_equal, T.xu3[R, 4:5], op.mult)
-        for k in range(1, N):
-            wf("ts", T.sg3[R, W * k:W * k + W], T.k3[R, :], float(k), op.is_equal, T.xu3[R, 5 * k + 4:5 * k + 5], op.mult)
-        yield
-        w("tt", T.sa3[R, :], T.sg3[R, 0:2 * W], T.sg3[R, 2 * W:4 * W], op.add)
-        wf("tt", T.sc3[R, :], T.sg3[R, 4 * W:5 * W], T.pl3[R, :], op.add)
-        yield
-        w("tt", T.sb3[R, :], T.sa3[R, 0:W], T.sa3[R, W:2 * W], op.add)
-        yield
-        mark["v3"] = w("tt", T.v3[R, :], T.sb3[R, :], T.sc3[R, :], op.add)
-    steps = third()
-
-    def step(n=1):
-        for _ in range(n):
-            if next(steps, 1) is not None:
-                return
-
-    V.wait_ge(S.d_e2, 96)
+    wf("ms", T.cs2[:, 1:50:10], 0.0)
     V.wait_ge(S.gd, cnt["gd"])
-    V.wait_ge(S.w, cnt["w"])
-    v("ts", T.cm2[R, :], T.e2[R, :], T.ct2[R, 0:1], op.is_ge)
-    step()
-    v("red", T.sg2[R, :], T.cm2[R, :], X, op.add)
-    step()
-    v("ts", T.bm2[R, :], T.ones[R, 0:32], T.sg2[R, 0:1], op.mult, T.ct2[R, 32:33], op.subtract)
-    for a in range(1, 4):
-        vf("ts", T.bm2[32 * a:32 * a + 30, :], T.ones[R, 0:32], T.sg2[R, 0:1], op.mult, T.ct2[R, 32:33], op.subtract)
-    step()
-    nrow = v("tr", T.row2[:], T.bm2[:])
-    A.wait_ge(S.v, nrow)
-    for k in range(N):
-        act(True, T.cx3[:, k, :], T.row2[0:32, 5 * me:5 * me + 10], LINE, scale=-0.2, bias=(386 - k) * 0.2)
-    mark["nc3"] = act(False, T.cr3[:], T.cx3[:], LINE, bias=float(WHOLE))
-    step()
-    v("ts", T.ci2[:], T.row2[:, 0:30], -0.2, op.mult, (386 - me) * 0.2, op.add)
-    step()
-    v("tt", T.cn2[:], T.ci2[:, 5:30], T.ci2[:, 0:25], op.subtract)
-    vf("tt", T.sh2[:], T.ci2[:, 4:29], T.rst[:, 0:25], op.mult)
-    step()
-    v("scan", T.cu2[:], T.rst[:, 0:25], T.cn2[:], 0.0, op.mult, op.add)
-    nde = vf("tt", T.de2[:], T.ci2[:, 0:25], T.sh2[:], op.subtract)
-    step()
-    V.wait_ge(S.v, nde)
-    A.wait_ge(S.v, nde)
-    for r in range(N):
-        for d in range(N):
-            out, e = T.seg[:, 25 * d + r:25 * d + 25:5], T.de2[:, 5 * d + r:5 * d + r + 1]
-            if r == 0:
-                nsg = act(d > 0, out, T.tcw[:], LINE, bias=e)
-            else:
-                vf("ts", out, T.tcw[:], T.cu2[:, 5 * d + r - 1:5 * d + r], op.is_ge, e, op.mult)
-    step()
+    wf("ts", T.bb3[R, 0:30], T.lst[R, :], float(W), op.mult)
+    wf("ms", T.bb3[:, 30:32], 0.0)
+    wf("ms", T.bb3[:, 32:96], 1.0)
+    wf("ts", T.mx[R, :], T.mr[R, :], -40.0, op.mult)
     V.wait_ge(S.ac, nsg)
-    v("scan", T.ss2[:], T.rst[:], T.seg[:], 0.0, op.mult, op.add)
-    step()
-    n2 = v("ts", T.l2[:, 0:25], T.ss2[:, 4:125:5], float(SLOT * (N - 1) + SENT1 - 1), op.min)
-    step()
+    for a in range(2, 4):
+        vf("ts", T.bm2[32 * a:32 * a + 30, :], T.ones[R, 0:32], T.sg2[R, 0:1], op.mult, T.run_c[R, 0:1], op.add)
+    V.wait_ge(S.ac, nbm)
+    v("tr", T.row2[:], T.bm2[:])
+    v("tt", T.nn2[:], T.row2[:, 0:25], T.row2[:, 5:30], op.subtract)
+    vf("ts", T.ci2[:], T.row2[:, 0:25], -0.1, op.mult, 38.8 - 0.2 * me, op.add)
+    v("ts", T.cs2[:, 2:50:2], T.nn2[:, 0:24], 0.1, op.mult, 128.4, op.add)
+    V.wait_ge(S.ac, nla)
+    wf("tr", T.aa3[:, 0:32], T.la3[:])
+    V.wait_ge(S.w, cnt["w"] - 1)
+    v("scan", T.o2[:], T.rst2[:], T.cs2[:], 0.0, op.mult, op.add)
+    ng3 = w("scan", T.g3[R, :], T.aa3[R, :], T.bb3[R, :], 0.0, op.add, op.add)
+    noff = v("tt", T.off2[:], T.ci2[:], T.o2[:, 1:50:2], op.subtract)
+    vf("tt", T.xo3[R, 0:5], T.row2[R, 5 * me:5 * me + 5], T.mx[R, :], op.mult)
+    nxo = vf("tt", T.xo3[R, 5:10], T.o2[R, 10 * me + 1:10 * me + 10:2], T.mr[R, :], op.mult)
+    nqq = w("ts", T.qq3[R, :], T.g3[R, 32:96], 0.1, op.mult, -0.6, op.add)
+    A.wait_ge(S.w, ng3)
+    ngv = act(T.gv3[R, :], T.g3[R, 32:96], LINE, scale=40.0, bias=15080.0)
+    A.wait_ge(S.v, nxo)
+    ncp = act(T.jk3[R, 0:5], T.xo3[R, 0:5], LINE, scale=0.0025, bias=7.56, accum_out=T.cp3[R, 0:1])
+    ncv = act(T.jk3[R, 5:15], T.xo3[R, :], LINE, accum_out=T.cv3[R, 0:1])
+    for j in range(N):
+        nfx = act(T.fx2[:, 25 * j:25 * j + 25], T.off2[:], LINE, bias=T.tcw[:, j:j + 1])
+    for j in range(N):
+        vf("ts", T.gx2[:, 25 * j:25 * j + 25], T.o2[:, 1:50:2], -STEP, op.mult, T.tcb[:, j:j + 1], op.add)
+    V.wait_ge(S.ac, ncp)
+    npp = wf("ts", T.pp3[R, :], T.g3[R, 32:96], 0.1, op.mult, T.cp3[R, 0:1], op.add)
+    V.wait_ge(S.w, nqq)
+    wf("tt", T.ts3[R, :], T.gv3[R, :], T.qq3[R, :], op.add)
+    V.wait_ge(S.w, npp)
+    V.wait_ge(S.ac, ncv)
+    wf("ts", T.tp3[R, :], T.pp3[R, :], -400.0, op.mult, T.cv3[R, 0:1], op.add)
+    V.wait_ge(S.ac, nfx)
+    v("scan", T.ss2[:], T.gx2[:], T.fx2[:], 0.0, op.max, op.min)
+    nv3 = w("tt", T.v3[R, :], T.tp3[R, :], T.ts3[R, :], op.add)
+    V.wait_ge(S.v, cnt["v"])
+    for j in range(N):
+        n2 = vf("ts", T.l2[:, j:25:5], T.ss2[:, 25 * j + 4:25 * j + 25:5], float(SLOT * (N - 1) + SENT1 - 1), op.min)
 
+    V.wait_ge(S.v, n2)
     V.wait_ge(S.s1c, landed)
     V.wait_ge(S.d_o1, 32)
     k2 = v("cp", T.q3[:].bitcast(dt.uint32), T.ql[:].bitcast(dt.uint32).indirect(T.l2[:, 0:25]))
@@ -304,29 +285,42 @@ def rank_program(g, core, T, topo):
     spread(lambda r: T.q3[:, cut(r, SLOT)].bitcast(dt.uint8), T.qm[:, cut(me, SLOT)].bitcast(dt.uint8), S.s2c)
     g.wait_ge(S.ap, 2)
     spread(lambda r: T.p3[:, cut(r, SLOT)], T.pm[:, cut(me, SLOT)], S.s2p)
+    g.sync.wait_ge(S.w, nv3)
+    g.sync.dma_start(T.val3[0:96:16, :], T.v3[R, :]).then_inc(S.d_v3, 16)
     g.sync.wait_ge(S.v, k2)
     g.sync.dma_start(T.qm[:, cut(me, SLOT)].bitcast(dt.uint8), T.q3[:, cut(me, SLOT)].bitcast(dt.uint8)).then_inc(S.d_o2, 16)
     g.sync.wait_ge(S.ap, 2)
     g.sync.dma_start(T.pm[:, cut(me, SLOT)], T.p3[:, cut(me, SLOT)]).then_inc(S.d_o2, 16)
 
-    step(99)
-    g.sync.wait_ge(S.w, mark["v3"])
-    g.sync.dma_start(T.val3[0:80:16, :], T.v3[R, :]).then_inc(S.d_v3, 16)
+    V.wait_ge(S.d_t3, 128)
+    nt0 = wf("tr", T.tr0[:], T.t3[:])
     V.wait_ge(S.d_w, 16)
-    w("qz", T.wq[:], T.wp[:], T.wt[:])
+    wf("qz", T.wq[:], T.wp[:], T.wt[:])
+    mine = COLS * me
+    wf("ms", T.win3[:, mine:mine + COLS], 0.0)
+    V.wait_ge(S.w, nt0)
+    wf("cp", T.of3[:], T.tr0[:, 0:20])
     V.wait_ge(S.d_v3, 16)
-    w("cp", T.win3[:].indirect(T.of3[:]), T.val3[:])
-    mine = T.win3[:, COLS * me:COLS * me + COLS]
-    w("cp", T.dup3[:, :, 0:16], mine)
-    wf("cp", T.dup3[:, :, 16:32], mine)
-    w("tr", T.tr3[:], T.dup3[:])
-    V.wait_ge(S.w, cnt["w"])
-    for r in range(N):
-        wf("cp", T.su3[:, r:120:5], T.tr3[32 * (r // 2):32 * (r // 2) + 32, 16 * (r % 2):768:32])
-    w("scan", T.sv3[:], T.rst[0:32, 0:120], T.su3[:], 0.0, op.mult, op.add)
-    w("ts", T.l3[0:32, :], T.sv3[:, 4:120:5], 200.0, op.add)
+    nw3 = w("cp", T.win3[:].indirect(T.of3[:]), T.val3[:])
+    A.wait_ge(S.w, nw3)
+    nd3 = act(T.dup3[:, 12:24, 16:32], T.win3[:, mine + 192:mine + 384], COPY)
+    w("cp", T.dup3[:, :, 0:16], T.win3[:, mine:mine + 384])
+    wf("cp", T.dup3[:, 0:12, 16:32], T.win3[:, mine:mine + 192])
+    V.wait_ge(S.ac, nd3)
+    nt3 = w("tr", T.tr3[:], T.dup3[:])
+    A.wait_ge(S.w, nt3)
+    V.wait_ge(S.w, nt3)
+    for r in range(H):
+        out, in_ = T.su3[:, r:144:6], T.tr3[32 * (r // 2):32 * (r // 2) + 32, 16 * (r % 2):768:32]
+        if r < 3:
+            wf("cp", out, in_)
+        else:
+            nsu = act(out, in_, COPY)
+    V.wait_ge(S.ac, nsu)
+    w("scan", T.sv3[:], T.rst6[:], T.su3[:], 0.0, op.mult, op.add)
+    w("ts", T.l3[0:32, :], T.sv3[:, 5:144:6], 200.0, op.add)
     for a in range(1, 4):
-        n3 = wf("ts", T.l3[32 * a:32 * a + 32, :], T.sv3[:, 4:120:5], 200.0, op.add)
+        n3 = wf("ts", T.l3[32 * a:32 * a + 32, :], T.sv3[:, 5:144:6], 200.0, op.add)
 
     V.wait_ge(S.s2c, landed)
     V.wait_ge(S.d_o2, 32)
@@ -338,7 +332,7 @@ def rank_program(g, core, T, topo):
     for h in range(2):
         c = slice(HALF * h, HALF * h + HALF)
         off = T.l3[:, 12 * h:12 * h + 12]
-        nk = vec("v", h > 0, "cp", (T.q4[:, c].bitcast(dt.uint32), T.qm[:].bitcast(dt.uint32).indirect(off)))
+        nk = vf("cp", T.q4[:, c].bitcast(dt.uint32), T.qm[:].bitcast(dt.uint32).indirect(off))
         A.activation(T.p4[:, c], T.pm[:].indirect(off), COPY).then_inc(S.ap, 1)
         g.tensor.wait_ge(S.v, nk)
         g.tensor.wait_ge(S.ap, 3 + h)
@@ -353,15 +347,16 @@ def rank_program(g, core, T, topo):
             out = T.y[:, COLS * o + HALF * h:COLS * o + HALF * h + HALF]
             if o == 0:
                 V.wait_ge(S["m%d" % b], 1)
-                ny = v("cp", y, T.ps[:, 512 * b:512 * b + HALF])
+                ny = vf("cp", y, T.ps[:, 512 * b:512 * b + HALF])
                 g.sync.wait_ge(S.v, ny)
                 g.sync.dma_start(out, y).then_inc(S.st, 16)
             else:
                 A.wait_ge(S["m%d" % b], 1)
-                act(False, y, T.ps[:, 512 * b:512 * b + HALF], COPY)
-                A.wait_ge(S.ac, cnt["ac"])
+                ny = act(y, T.ps[:, 512 * b:512 * b + HALF], COPY)
+                A.wait_ge(S.ac, ny)
                 A.dma_start(out, y).then_inc(S.st2, 16)
     g.sync.wait_ge(S.st, 32)
     A.wait_ge(S.st2, 32)
     g.wait_ge(S.v, cnt["v"])
+    g.wait_ge(S.w, cnt["w"])
     g.wait_ge(S.loc, 5 * landed)

from concourse.bass import DstId, RemoteDMATransfer
from concourse.mybir import dt, AluOpType, ActivationFunctionType

N, COLS = 5, 384
SLOT = 80
SENT1 = 78
H = 6
W = COLS // H
STEP = 1024.0

F32, BF, I32, U16 = "float32", "bfloat16", "int32", "uint16"
X4, U8 = "float8_e4m3fn_x4", "uint8"
SMALL = {
    X4: "q:128,384 wq:128,256 q2:128,400 ql:128,400 q3:128,400 qm:128,400 q4:128,384",
    U8: "p:128,384 wp:128,256 p2:128,400 pl:128,400 p3:128,400 pm:128,400 p4:128,384",
    BF: "xt:128,1536 wt:128,1024 nat:128,6,64 val1:128,192 win1:128,400 dup1:128,25,32 tr1:128,800 v3:32,64 val3:128,320 "
        "win3:128,1920 dup3:128,24,32 tr3:128,768 cs2:128,50",
    I32: "l0:16,24 e1:32,64 ci2:128,25 pp3:32,64 qq3:32,64",
    U16: "of1:128,12 l1:128,26 l2:128,26 of3:128,20 l3:128,24",
    F32: "ys:128,768 lf:16,24 lo_r:32,35 key_r:32,35 thr_r:32,35 run_r:32,35 q_r:128,32 lo_c:32,32 key_c:32,32 thr_c:32,32 "
         "run_c:32,32 q_c:128,32 ones:128,144 rst:128,125 rst6:32,144 rst2:128,50 tc0:128,5 tcw:128,5 tcb:128,5 lm:32,32 sa0:32,30 "
         "sam:32,30 lsa:32,30 lst:32,30 mr0:32,5 mr:32,5 mx:32,5 ab0:32,96 ab1:32,96 c1:32,64 ln1:32,32 g1:32,96 z1:32,64 zt1:32,64 "
         "s1:32,60 sm1:128,25 e2:32,384 jk2:32,384 sg2:32,1 bm2:128,32 row2:128,32 nn2:128,25 o2:128,50 off2:128,25 gx2:128,125 "
         "fx2:128,125 ss2:128,125 e3:32,64 u3:32,64 na3:32,1 la3:32,32 aa3:32,96 bb3:32,96 g3:32,96 gv3:32,64 xo3:32,10 jk3:32,16 "
         "cp3:32,1 cv3:32,1 tp3:32,64 ts3:32,64 t3:128,32 tr0:128,32 su3:32,144 sv3:32,144",
}
SCRATCH = {"ps": ("psum", [128, 2048], F32), "lists": ("dram", [N, 128, 3], F32)}
for _t in SMALL:
    for _b in SMALL[_t].split():
        SCRATCH[_b.split(":")[0]] = ("sbuf", [int(_n) for _n in _b.split(":")[1].split(",")], _t)
SEMAPHORES = ["v", "w", "ac", "ap", "ga", "gb", "gn", "ge", "gd", "d_e1", "d_x", "d_w", "d_l", "d_lf", "d_e2", "d_e3", "d_t3",
              "d_o1", "d_v1", "d_v3", "d_o2", "sl", "s1c", "s1p", "s2c", "s2p", "loc", "m0", "m1", "m2", "m3", "st", "st2"]


def rank_program(g, core, T, topo):
    me = T.rank_of(core)
    if me is None:
        return
    S, V, A = T.sem, g.vector, g.scalar
    op, FN = AluOpType, ActivationFunctionType
    COPY, LINE = FN.Copy, FN.Identity
    others = [r for r in range(N) if r != me]
    cnt = {"v": 0, "w": 0, "ac": 0, "ga": 0, "gb": 0, "gn": 0, "ge": 0, "gd": 0}
    CALL = {"ts": V.tensor_scalar, "tt": V.tensor_tensor, "cp": V.tensor_copy, "ms": V.memset,
            "scan": V.tensor_tensor_scan, "tr": V.transpose, "qz": V.quantize_mx}

    def vec(line, free, name, args):
        if cnt[line] and not free:
            V.wait_ge(S[line], cnt[line])
        if name == "ts":
            out, a, s1, o1 = args[:4]
            args = (out, a, s1, None, o1) if len(args) == 4 else (out, a, s1, args[4], o1, args[5])
        CALL[name](*args).then_inc(S[line], 1)
        cnt[line] += 1
        return cnt[line]
    v = lambda name, *args: vec("v", False, name, args)
    vf = lambda name, *args: vec("v", True, name, args)
    w = lambda name, *args: vec("w", False, name, args)
    wf = lambda name, *args: vec("w", True, name, args)

    def act(out, in_, func, **k):
        A.activation(out, in_, func, **k).then_inc(S.ac, 1)
        cnt["ac"] += 1
        return cnt["ac"]

    def iota(line, out, pattern, base=0, cm=0):
        g.iota(out, pattern, base, cm, allow_small_or_imprecise_dtypes=True).then_inc(S[line], 1)
        cnt[line] += 1

    def sel(line, out, in_, pattern, how, base, cm):
        g.affine_select(out, in_, pattern, how, 0.0, base, cm).then_inc(S[line], 1)
        cnt[line] += 1
    R = slice(0, 30)

    g.sync.dma_start(T.l0[:], T.to[:]).then_inc(S.d_l, 16)
    for d in range(N):
        (g.sync if d % 2 else A).dma_start(T.e1[d:N * H:N, :], T.to[:]).then_inc(S.d_e1, 16)
    g.sync.dma_start(T.xt[:, 0:768], T.x[:, 0:768]).then_inc(S.d_x, 16)
    A.dma_start(T.xt[:, 768:1536], T.x[:, 768:1536]).then_inc(S.d_x, 16)
    A.dma_start(T.wt[:], T.w[:]).then_inc(S.d_w, 16)

    iota("ga", T.lo_r[:], [[0, H + 1], [COLS, N]])
    iota("ga", T.key_r[:], [[1, H + 1], [H, N]])
    nones = vf("ms", T.ones[:], 1.0)
    for b in ("z1", "ln1"):
        vf("ms", T[b][:], 0.0)
    vf("ms", T.ab1[:, 0:32], 0.0)
    vf("ms", T.val1[:], 0.0)
    V.wait_ge(S.ga, cnt["ga"])
    vf("tr", T.lo_c[:], T.lo_r[:, 0:32])
    vf("tr", T.key_c[:], T.key_r[:, 0:32])
    v("ts", T.lm[R, :], T.key_r[R, 0:32], T.key_c[R, 0:1], op.is_gt)
    wf("ms", T.val3[:], 0.0)
    iota("gn", T.nat[:], [[1, 16], [16, 24]], -192)
    g.wait_ge(S.v, nones)
    sel("gb", T.rst[:], T.ones[:, 0:125], [[0, 25], [1, 5]], op.is_gt, 0, 0)

    V.wait_ge(S.d_e1, 80)
    v("ts", T.ab0[R, 32:96], T.e1[R, :], T.lo_c[R, 0:1], op.is_ge)
    nab = vf("ts", T.ab1[R, 32:96], T.e1[R, :], -float(COLS), op.add, T.lo_c[R, 0:1], op.is_ge)
    V.wait_ge(S.d_l, 16)
    nlf = wf("cp", T.lf[:], T.l0[:])
    g.sync.wait_ge(S.w, nlf)
    g.sync.dma_start(T.lists[me], T.lf[:]).then_inc(S.d_lf, 16)
    g.sync.wait_ge(S.v, nab)
    g.sync.wait_ge(S.gn, cnt["gn"])
    for blk in range(2):
        for odd in range(2):
            g.sync.dma_start(T.val1[16 * odd:128:32, 96 * blk:96 * blk + 96],
                             T.nat[16 * odd:128:32, :, 32 * blk + 16 * odd:32 * blk + 16 * odd + 16]).then_inc(S.d_v1, 16)

    per = len(topo.engines(core, T.cores[others[0]])) // len(others)
    landed = per * len(others)

    def spread(src, dst, sem):
        moves = []
        for i, r in enumerate(others):
            rid, pid, _ = topo.addr(T.cores[r])
            e = topo.engines(core, T.cores[r])[per * i:per * i + per]
            moves.append(RemoteDMATransfer(dst_ids=[DstId(rid=rid, pnc=pid)], dma_engine_mask=sum(1 << b for b in e),
                                           remote_sem=sem, srcs=[src(r)], dsts=[dst]))
        g.remote_dma_fused(moves, local_sem=S.loc)

    iota("ge", T.thr_r[:], [[-2 * COLS, H + 1], [0, N]], 1)
    iota("ge", T.run_r[:], [[0, H + 1], [-10 * SLOT, N]])
    iota("ge", T.q_r[:], [[0, 2], [1, 16]])
    iota("ge", T.tc0[:], [[16, 5]])
    g.wait_ge(S.d_lf, 16)
    spread(lambda r: T.lists[me], T.lists[me], S.sl)

    sel("gd", T.sa0[:], T.ones[0:32, 0:30], [[-H, 5], [0, H]], op.is_ge, 0, 1)
    sel("gd", T.mr0[:], T.ones[0:32, 0:5], [[-H, 5]], op.is_ge, 0, 1)
    sel("gd", T.rst2[:], T.ones[:, 0:50], [[0, 5], [1, 10]], op.not_equal, -1, 0)
    g.wait_ge(S.gd, cnt["gd"])
    sel("gd", T.sam[:], T.sa0[:], [[H, 5], [0, H]], op.is_ge, H - 1, -1)
    sel("gd", T.mr[:], T.mr0[:], [[H, 5]], op.is_ge, H - 1, -1)
    g.wait_ge(S.gd, cnt["gd"])
    sel("gd", T.lsa[:], T.sam[:], [[1, 30]], op.is_gt, 0, -1)
    sel("gd", T.lst[:], T.sam[:], [[-1, 30]], op.is_gt, 0, 1)
    sel("gd", T.rst6[:], T.ones[0:32, :], [[0, 24], [1, H]], op.is_gt, 0, 0)

    v("scan", T.c1[R, :], T.ab0[R, 32:96], T.ab1[R, 32:96], 0.0, op.add, op.subtract)
    wf("ms", T.win1[:, 0:200], 0.0)
    v("ts", T.ln1[R, :], T.lm[R, :], T.c1[R, W - 1:W], op.mult)
    wf("ms", T.win1[:, 200:400], 0.0)
    v("tr", T.ab0[:, 0:32], T.ln1[:])
    for b in ("t3", "bm2", "la3"):
        wf("ms", T[b][:], 0.0)
    nz = cnt["w"]
    v("scan", T.g1[R, :], T.ab0[R, :], T.ab1[R, :], 0.0, op.add, op.subtract)

    def pack(b):
        return wf("qz", T.q[:, 128 * b:128 * b + 128], T.p[:, 128 * b:128 * b + 128], T.xt[:, 512 * b:512 * b + 512])
    V.wait_ge(S.d_x, 32)
    pack(0)
    v("tt", T.z1[R, :], T.g1[R, 32:96], T.ab0[R, 32:96], op.mult)
    pack(1)
    v("tr", T.zt1[:], T.z1[:])
    n1 = pack(2)
    V.wait_ge(S.gb, cnt["gb"])
    v("scan", T.s1[:, 0:30], T.rst[0:32, 0:30], T.zt1[:, 0:30], 0.0, op.mult, op.max)
    vf("scan", T.s1[:, 30:60], T.rst[0:32, 0:30], T.zt1[:, 32:62], 0.0, op.mult, op.max)
    wf("ms", T.cs2[:], -128.0)
    v("ts", T.of1[0:32, :], T.s1[:, 4:60:5], -1.0, op.add)
    for a in range(1, 4):
        vf("ts", T.of1[32 * a:32 * a + 32, :], T.s1[:, 4:60:5], -1.0, op.add)
    V.wait_ge(S.w, n1)
    V.wait_ge(S.d_v1, 64)
    nw1 = v("cp", T.win1[:, 0:400].indirect(T.of1[:, 0:12]), T.val1[:])
    A.wait_ge(S.v, nw1)
    V.wait_ge(S.ge, cnt["ge"])
    nct = wf("tr", T.thr_c[:], T.thr_r[:, 0:32])
    V.wait_ge(S.v, nw1)
    for k in range(N):
        for u in (0, 16):
            out, in_ = T.dup1[:, 5 * k:5 * k + 5, u:u + 16], T.win1[:, k:400:5]
            if k < 3:
                vf("cp", out, in_)
            else:
                nd1 = act(out, in_, COPY)
    V.wait_ge(S.ac, nd1)
    v("tr", T.tr1[:], T.dup1[:])
    wf("tr", T.q_c[:], T.q_r[:])
    nrc = wf("tr", T.run_c[:], T.run_r[:, 0:32])
    v("tt", T.sm1[:], T.tr1[:, 0:800:32], T.tr1[:, 16:800:32], op.add)
    w("ts", T.tcw[:], T.tc0[:], T.q_c[:, 0:1], op.add)
    nl1 = v("ts", T.l1[:, 0:25], T.sm1[:], 192.0, op.add)
    w("ts", T.tcb[:], T.tcw[:], 0.5, op.add, STEP, op.mult)
    k1 = v("cp", T.q2[:].bitcast(dt.uint32), T.q[:].bitcast(dt.uint32).indirect(T.l1[:, 0:25]))
    A.wait_ge(S.w, n1)
    A.wait_ge(S.v, nl1)
    A.activation(T.p2[:], T.p[:].indirect(T.l1[:, 0:25]), COPY).then_inc(S.ap, 1)

    cut = lambda r, n: slice(SLOT * r, SLOT * r + n)
    g.wait_ge(S.v, k1)
    spread(lambda r: T.q2[:, cut(r, SENT1)].bitcast(dt.uint8), T.ql[:, cut(me, SENT1)].bitcast(dt.uint8), S.s1c)
    g.wait_ge(S.ap, 1)
    spread(lambda r: T.p2[:, cut(r, SENT1)], T.pl[:, cut(me, SENT1)], S.s1p)

    g.sync.wait_ge(S.w, nz)
    g.sync.wait_ge(S.sl, landed)
    g.sync.wait_ge(S.d_lf, 16)
    for d in range(N + 1):
        g.sync.dma_start(T.e2[N * d:N * d + N, :], T.lists[:]).then_inc(S.d_e2, 16)
    g.sync.dma_start(T.e3[R, :], T.lists[:]).then_inc(S.d_e3, 16)
    g.sync.wait_ge(S.d_e3, 16)
    for b in range(8):
        g.sync.dma_start(T.t3[32 * (b // 2):32 * (b // 2) + 20, 16 * (b % 2):16 * (b % 2) + 16],
                         T.e3[5 * (b % H):5 * (b % H) + 5, :]).then_inc(S.d_t3, 16)
    g.sync.wait_ge(S.v, k1)
    g.sync.dma_start(T.ql[:, cut(me, SLOT)].bitcast(dt.uint8), T.q2[:, cut(me, SLOT)].bitcast(dt.uint8)).then_inc(S.d_o1, 16)
    g.sync.wait_ge(S.ap, 1)
    g.sync.dma_start(T.pl[:, cut(me, SLOT)], T.p2[:, cut(me, SLOT)]).then_inc(S.d_o1, 16)

    A.wait_ge(S.d_e2, 96)
    A.wait_ge(S.w, nct)
    nsg = act(T.jk2[R, :], T.e2[R, :], FN.Sign, scale=2.0, bias=T.thr_c[R, 0:1], accum_out=T.sg2[R, 0:1])
    A.wait_ge(S.d_e3, 16)
    nu3 = act(T.u3[R, :], T.e3[R, :], FN.Abs, scale=2.0, bias=-float(2 * COLS * me + COLS - 1))
    A.wait_ge(S.ac, nsg)
    A.wait_ge(S.w, nrc)
    for a in range(2):
        nbm = act(T.bm2[32 * a:32 * a + 30, :], T.ones[R, 0:32], LINE, scale=T.sg2[R, 0:1], bias=T.run_c[R, 0:1])
    A.wait_ge(S.ac, nu3)
    ni3 = act(T.aa3[R, 32:96], T.u3[R, :], FN.Sign, scale=-1.0, bias=float(COLS), accum_out=T.na3[R, 0:1])
    A.wait_ge(S.gd, cnt["gd"])
    A.wait_ge(S.ac, ni3)
    nla = act(T.la3[R, 0:30], T.lsa[R, :], LINE, scale=T.na3[R, 0:1])

    wf("ms", T.cs2[:, 1:50:10], 0.0)
    V.wait_ge(S.gd, cnt["gd"])
    wf("ts", T.bb3[R, 0:30], T.lst[R, :], float(W), op.mult)
    wf("ms", T.bb3[:, 30:32], 0.0)
    wf("ms", T.bb3[:, 32:96], 1.0)
    wf("ts", T.mx[R, :], T.mr[R, :], -40.0, op.mult)
    V.wait_ge(S.ac, nsg)
    for a in range(2, 4):
        vf("ts", T.bm2[32 * a:32 * a + 30, :], T.ones[R, 0:32], T.sg2[R, 0:1], op.mult, T.run_c[R, 0:1], op.add)
    V.wait_ge(S.ac, nbm)
    v("tr", T.row2[:], T.bm2[:])
    v("tt", T.nn2[:], T.row2[:, 0:25], T.row2[:, 5:30], op.subtract)
    vf("ts", T.ci2[:], T.row2[:, 0:25], -0.1, op.mult, 38.8 - 0.2 * me, op.add)
    v("ts", T.cs2[:, 2:50:2], T.nn2[:, 0:24], 0.1, op.mult, 128.4, op.add)
    V.wait_ge(S.ac, nla)
    wf("tr", T.aa3[:, 0:32], T.la3[:])
    V.wait_ge(S.w, cnt["w"] - 1)
    v("scan", T.o2[:], T.rst2[:], T.cs2[:], 0.0, op.mult, op.add)
    ng3 = w("scan", T.g3[R, :], T.aa3[R, :], T.bb3[R, :], 0.0, op.add, op.add)
    noff = v("tt", T.off2[:], T.ci2[:], T.o2[:, 1:50:2], op.subtract)
    vf("tt", T.xo3[R, 0:5], T.row2[R, 5 * me:5 * me + 5], T.mx[R, :], op.mult)
    nxo = vf("tt", T.xo3[R, 5:10], T.o2[R, 10 * me + 1:10 * me + 10:2], T.mr[R, :], op.mult)
    nqq = w("ts", T.qq3[R, :], T.g3[R, 32:96], 0.1, op.mult, -0.6, op.add)
    A.wait_ge(S.w, ng3)
    ngv = act(T.gv3[R, :], T.g3[R, 32:96], LINE, scale=40.0, bias=15080.0)
    A.wait_ge(S.v, nxo)
    ncp = act(T.jk3[R, 0:5], T.xo3[R, 0:5], LINE, scale=0.0025, bias=7.56, accum_out=T.cp3[R, 0:1])
    ncv = act(T.jk3[R, 5:15], T.xo3[R, :], LINE, accum_out=T.cv3[R, 0:1])
    for j in range(N):
        nfx = act(T.fx2[:, 25 * j:25 * j + 25], T.off2[:], LINE, bias=T.tcw[:, j:j + 1])
    for j in range(N):
        vf("ts", T.gx2[:, 25 * j:25 * j + 25], T.o2[:, 1:50:2], -STEP, op.mult, T.tcb[:, j:j + 1], op.add)
    V.wait_ge(S.ac, ncp)
    npp = wf("ts", T.pp3[R, :], T.g3[R, 32:96], 0.1, op.mult, T.cp3[R, 0:1], op.add)
    V.wait_ge(S.w, nqq)
    wf("tt", T.ts3[R, :], T.gv3[R, :], T.qq3[R, :], op.add)
    V.wait_ge(S.w, npp)
    V.wait_ge(S.ac, ncv)
    wf("ts", T.tp3[R, :], T.pp3[R, :], -400.0, op.mult, T.cv3[R, 0:1], op.add)
    V.wait_ge(S.ac, nfx)
    v("scan", T.ss2[:], T.gx2[:], T.fx2[:], 0.0, op.max, op.min)
    nv3 = w("tt", T.v3[R, :], T.tp3[R, :], T.ts3[R, :], op.add)
    V.wait_ge(S.v, cnt["v"])
    for j in range(N):
        n2 = vf("ts", T.l2[:, j:25:5], T.ss2[:, 25 * j + 4:25 * j + 25:5], float(SLOT * (N - 1) + SENT1 - 1), op.min)

    V.wait_ge(S.v, n2)
    V.wait_ge(S.s1c, landed)
    V.wait_ge(S.d_o1, 32)
    k2 = v("cp", T.q3[:].bitcast(dt.uint32), T.ql[:].bitcast(dt.uint32).indirect(T.l2[:, 0:25]))
    A.wait_ge(S.v, n2)
    A.wait_ge(S.s1p, landed)
    A.wait_ge(S.d_o1, 32)
    A.activation(T.p3[:], T.pl[:].indirect(T.l2[:, 0:25]), COPY).then_inc(S.ap, 1)
    g.wait_ge(S.v, k2)
    spread(lambda r: T.q3[:, cut(r, SLOT)].bitcast(dt.uint8), T.qm[:, cut(me, SLOT)].bitcast(dt.uint8), S.s2c)
    g.wait_ge(S.ap, 2)
    spread(lambda r: T.p3[:, cut(r, SLOT)], T.pm[:, cut(me, SLOT)], S.s2p)
    g.sync.wait_ge(S.w, nv3)
    g.sync.dma_start(T.val3[0:96:16, :], T.v3[R, :]).then_inc(S.d_v3, 16)
    g.sync.wait_ge(S.v, k2)
    g.sync.dma_start(T.qm[:, cut(me, SLOT)].bitcast(dt.uint8), T.q3[:, cut(me, SLOT)].bitcast(dt.uint8)).then_inc(S.d_o2, 16)
    g.sync.wait_ge(S.ap, 2)
    g.sync.dma_start(T.pm[:, cut(me, SLOT)], T.p3[:, cut(me, SLOT)]).then_inc(S.d_o2, 16)

    V.wait_ge(S.d_t3, 128)
    nt0 = wf("tr", T.tr0[:], T.t3[:])
    V.wait_ge(S.d_w, 16)
    wf("qz", T.wq[:], T.wp[:], T.wt[:])
    mine = COLS * me
    wf("ms", T.win3[:, mine:mine + COLS], 0.0)
    V.wait_ge(S.w, nt0)
    wf("cp", T.of3[:], T.tr0[:, 0:20])
    V.wait_ge(S.d_v3, 16)
    nw3 = w("cp", T.win3[:].indirect(T.of3[:]), T.val3[:])
    A.wait_ge(S.w, nw3)
    nd3 = act(T.dup3[:, 12:24, 16:32], T.win3[:, mine + 192:mine + 384], COPY)
    w("cp", T.dup3[:, :, 0:16], T.win3[:, mine:mine + 384])
    wf("cp", T.dup3[:, 0:12, 16:32], T.win3[:, mine:mine + 192])
    V.wait_ge(S.ac, nd3)
    nt3 = w("tr", T.tr3[:], T.dup3[:])
    A.wait_ge(S.w, nt3)
    V.wait_ge(S.w, nt3)
    for r in range(H):
        out, in_ = T.su3[:, r:144:6], T.tr3[32 * (r // 2):32 * (r // 2) + 32, 16 * (r % 2):768:32]
        if r < 3:
            wf("cp", out, in_)
        else:
            nsu = act(out, in_, COPY)
    V.wait_ge(S.ac, nsu)
    w("scan", T.sv3[:], T.rst6[:], T.su3[:], 0.0, op.mult, op.add)
    w("ts", T.l3[0:32, :], T.sv3[:, 5:144:6], 200.0, op.add)
    for a in range(1, 4):
        n3 = wf("ts", T.l3[32 * a:32 * a + 32, :], T.sv3[:, 5:144:6], 200.0, op.add)

    V.wait_ge(S.s2c, landed)
    V.wait_ge(S.d_o2, 32)
    V.wait_ge(S.w, n3)
    A.wait_ge(S.w, n3)
    A.wait_ge(S.s2p, landed)
    A.wait_ge(S.d_o2, 32)
    HALF = COLS // 2
    for h in range(2):
        c = slice(HALF * h, HALF * h + HALF)
        off = T.l3[:, 12 * h:12 * h + 12]
        nk = vf("cp", T.q4[:, c].bitcast(dt.uint32), T.qm[:].bitcast(dt.uint32).indirect(off))
        A.activation(T.p4[:, c], T.pm[:].indirect(off), COPY).then_inc(S.ap, 1)
        g.tensor.wait_ge(S.v, nk)
        g.tensor.wait_ge(S.ap, 3 + h)
        for o in range(2):
            b = 2 * h + o
            g.tensor.matmul_mx(T.ps[:, 512 * b:512 * b + HALF], T.wq[:, 128 * o:128 * o + 128], T.wp[:, 128 * o:128 * o + 128],
                               T.q4[:, c], T.p4[:, c], True, True).then_inc(S["m%d" % b], 1)
    for h in range(2):
        for o in range(2):
            b = 2 * h + o
            y = T.ys[:, COLS * o + HALF * h:COLS * o + HALF * h + HALF]
            out = T.y[:, COLS * o + HALF * h:COLS * o + HALF * h + HALF]
            if o == 0:
                V.wait_ge(S["m%d" % b], 1)
                ny = vf("cp", y, T.ps[:, 512 * b:512 * b + HALF])
                g.sync.wait_ge(S.v, ny)
                g.sync.dma_start(out, y).then_inc(S.st, 16)
            else:
                A.wait_ge(S["m%d" % b], 1)
                ny = act(y, T.ps[:, 512 * b:512 * b + HALF], COPY)
                A.wait_ge(S.ac, ny)
                A.dma_start(out, y).then_inc(S.st2, 16)
    g.sync.wait_ge(S.st, 32)
    A.wait_ge(S.st2, 32)
    g.wait_ge(S.v, cnt["v"])
    g.wait_ge(S.w, cnt["w"])
    g.wait_ge(S.loc, 5 * landed)
